import numpy as np, ml_dtypes
CORES = [24,25,26,27,28,29,30,31]
N = 8
import mx_ref
BF = ml_dtypes.bfloat16
def cols(t, e):
    v = np.concatenate([t.reshape(128, -1, 4), np.zeros((128, 1, 4), BF)], axis=1)
    return np.ascontiguousarray(v[:, e]).reshape(128, -1)
def pick(q, e):
    c = np.concatenate([q[0].reshape(128, -1, 4), np.zeros((128, 1, 4), np.uint8)], axis=1); s = np.concatenate([q[1], np.ones((16, 1), np.uint8)], axis=1)
    return (np.ascontiguousarray(c[:, e].reshape(128, -1)), np.ascontiguousarray(s[:, e]))
def join(*qs):
    return (np.concatenate([q[0] for q in qs], axis=1), np.concatenate([q[1] for q in qs], axis=1))
def put(q, e, v):
    c, s = q[0].reshape(128, -1, 4).copy(), q[1].copy(); c[:, e] = v[0].reshape(128, -1, 4); s[:, e] = v[1]
    return (c.reshape(128, -1), s)
def pk(c, s):
    return (np.ascontiguousarray(c), mx_ref.live(s))
def emit(q):
    return q[0], q[1]
def decode(q):
    o = []
    for b in range(4):
        e = np.zeros((128, 128, 4), np.float32); e[np.arange(128), np.arange(128), b] = 1
        o.append(mx_ref.matmul(mx_ref.quantize(e.reshape(128, 512).astype(BF)), q))
    return np.stack(o, axis=2).reshape(128, -1)
def f(rng, *shape):
    return mx_ref.flush((rng.standard_normal(shape, dtype=np.float32) * np.exp2(rng.integers(-2, 3, shape[:-1] + (1,)))).astype(BF))
def wide(rng, *shape, cols=0):
    v = rng.standard_normal(shape, dtype=np.float32) * np.exp2(rng.integers(-12, 13, shape)).astype(np.float32)
    if cols: v *= np.repeat(np.exp2(rng.integers(-cols, cols + 1, shape[:-2] + (1, shape[-1] // 4))) * (rng.random(shape[:-2] + (1, shape[-1] // 4)) > 0.0625), 4, axis=-1).astype(np.float32)
    return mx_ref.flush(v.astype(BF))
T, L, PL, R = 256, 32, 5, 3
def sized(v, k):
    v = v.astype(np.float32) * np.float32(k)
    v[np.abs(v) < np.float32(2.0 ** -6)] = 0
    return v.astype(BF)
def column(w, k, v):
    w[:, :, 4 * k:4 * k + 4] = np.asarray(v, np.float32).astype(BF)
def plain(rng):
    return {"x": sized(f(rng, N, 128, 4 * T), 16), "w": np.repeat(f(rng, 1, 128, 512), N, axis=0), "z": f(rng, N, 128, 512)}
def setup_inputs(rng):
    return plain(rng)
def setup_inputs_steps(rng):
    d = plain(rng)
    d["w"][:, 96:] = 0
    for t in range(R):
        v = np.zeros((128, 4))
        v[0, 0], v[64, 0] = 1.0, 2.0 ** -21
        column(d["w"], 8 * t + 6, v)
        for i in range(PL): d["w"][:, 64, 4 * (8 * t + i)] = 0
    x = d["x"].reshape(N, 128, T, 4).astype(np.float32)
    x[:, :96] = np.tile(x[:, :96, :T // 4], (1, 1, 4, 1))
    x[:, 64, :, 0] = np.repeat([5.0, 6.0, 7.0, 7.0], T // 4)
    x[:, 0, :, 0] = np.where(np.arange(N) % 2 == 0, 4.0, -4.0)[:, None]
    d["x"] = x.reshape(N, 128, 4 * T).astype(BF)
    return d
def setup_inputs_far(rng):
    d = plain(rng)
    g = 1 - 2 * rng.integers(0, 2, (N, T))
    g[::2] = 1
    v = (1.5 + 0.5 * rng.random((N, 128, 4 * T), dtype=np.float32)) * np.float32(2.0 ** 27)
    d["x"] = (v * np.repeat(g, 4, axis=1)[:, None, :].astype(np.float32)).astype(BF)
    for t in range(R):
        for i in range(PL):
            column(d["w"], 8 * t + i, np.repeat([-1.0, 1.0], 256)[rng.permutation(512)].reshape(128, 4))
        column(d["w"], 8 * t + 6, -(2.0 ** 30) * rng.choice([0.875, 1.0], (128, 4)))
    return d
def setup_inputs_cancel(rng):
    d = plain(rng)
    d["w"][:, 64:] = 0
    d["x"][:, :64, :4] = d["x"][0, :64, :4].astype(np.float32).astype(BF)
    v = rng.integers(4, 8, (64, 4)) * 2.0 ** 22 * rng.choice([-1.0, 1.0], (64, 4))
    k = [1.0, 2.0 ** -26, -1.0, 2.0 ** -26]
    for r in range(N):
        d["x"][r, 64:] = np.tile(v * k[r % 4], (1, T)).astype(np.float32).astype(BF)
    return d
def setup_inputs_bare(rng):
    d = plain(rng)
    a, b = [int(i) for i in rng.permutation(N)[:2]]
    d["x"][:, 127, ::4] = 0
    one = d["x"][a, :, :4].astype(np.float32)
    k = np.repeat(np.exp2(rng.integers(0, 4, T)), 4).astype(np.float32)
    d["x"][a] = (np.tile(one, (1, T)) * k).astype(BF)
    e = np.where(rng.permutation(T) % 4 > 0, -1, np.arange(T))
    d["x"][b] = cols(d["x"][b], e)
    d["x"][b, 127, 4 * np.flatnonzero(e >= 0)] = 65536.0
    for i in range(PL): d["w"][:, 127, 4 * i] = 1.0
    d["w"][:, 127, 4 * 6] = -1.0
    for i in range(PL): column(d["w"], 8 + i, 0)
    column(d["w"], 8 * (R - 1) + 6, 0)
    return d
def setup_inputs_spread(rng):
    return {**plain(rng), "x": sized(wide(rng, N, 128, 4 * T, cols=6), 64)}
def check_inputs(d):
    b = []
    for k, low, high in (("x", 2.0 ** -6, 2.0 ** 28), ("w", 2.0 ** -30, 2.0 ** 30), ("z", 2.0 ** -30, 2.0 ** 30)):
        v = np.abs(d[k].astype(np.float32))
        if not (np.isfinite(v).all() and ((v == 0) | (v >= low) & (v <= high)).all()): b.append("a value of " + k)
    w = d["w"].astype(np.float32)
    if (w != w[:1]).any(): b.append("w differs from rank to rank")
    return b
def reference(x, w, z):
    y, lv = np.zeros((N, 128, T), np.float32), np.zeros((N, R, T), np.float32)
    oc, osc = np.zeros((N, 128, 4 * T), np.uint8), np.zeros((N, 16, T), np.uint8)
    state = [mx_ref.quantize(np.ascontiguousarray(x[r])) for r in range(N)]
    wq = [mx_ref.quantize(np.ascontiguousarray(w[r])) for r in range(N)]
    for t in range(R):
        leaf, have = np.zeros((N, T), int), []
        total = np.zeros((128, L, 4), np.float32)
        for r in range(N):
            p = mx_ref.matmul(wq[r], state[r])[8 * t:8 * t + 7] + np.float32(0)
            have.append(decode(state[r]).reshape(128, T, 4))
            for i in range(PL): leaf[r] += (p[i] < 0) * (1 << i)
            for l in range(L):
                m = np.flatnonzero(leaf[r] == l)
                if m.size: total[:, l] = total[:, l] + have[r][:, m[np.argmax(p[6, m])]]
        v = mx_ref.quantize(np.ascontiguousarray((total * np.float32(0.125)).reshape(128, 4 * L).astype(BF)))
        v = decode(v).reshape(128, L, 4)
        for r in range(N):
            new = have[r] - v[:, leaf[r]] * np.float32(0.5)
            state[r] = mx_ref.quantize(np.ascontiguousarray(new.reshape(128, 4 * T).astype(BF)))
            lv[r, t] = leaf[r]
    for r in range(N):
        y[r] = mx_ref.matmul(mx_ref.quantize(np.ascontiguousarray(z[r])), state[r])
        oc[r], osc[r] = emit(state[r])
    return {"y": y, "oc": oc, "osc": osc, "lv": lv}

@@ -1,0 +1,326 @@
+from concourse.bass import DstId, RemoteDMATransfer
+from concourse.mybir import dt, AluOpType, AxisListType, ActivationFunctionType
+
+R = 3
+TC = 256
+NL = 32
+Q8 = "float8_e4m3fn_x4"
+
+
+def _scratch():
+    s = {}
+    for name, cols in (("xin", 1032),
+                       ("ht", 1032),
+                       ("ut", 704),
+                       ("st", 1792),
+                       ("zin", 512), ("zz", 256),
+                       ("ct", 512),
+                       ("cl", 1024),
+                       ("fe", 520),
+                       ("ff", 520),
+                       ("rm8", 256), ("rm16", 256),
+                       ("bt", 512),
+                       ("vt", 1024)):
+        s[name] = ("sbuf", [128, cols], "bfloat16")
+    for name, cols in (("vi", 8), ("li", 64), ("fa", 8), ("fb", 8), ("sca", 4), ("scb", 4), ("yb", 64), ("db", 64),
+                       ("sel", 128), ("pf", 4), ("k2", 16), ("ssc", 128), ("score", 132), ("pm", 132), ("junk", 132),
+                       ("cnt", 4), ("g1", 4), ("g2", 4), ("lrow", 768), ("lm", 256), ("lsc", 256), ("yo", 256)):
+        s[name] = ("sbuf", [128, cols], "float32")
+    for name, cols in (("yi", 64), ("vb", 128), ("vm", 128), ("pint", 4), ("pa7", 4), ("pb1", 4)):
+        s[name] = ("sbuf", [128, cols], "int32")
+    for name, cols in (("coff", 16), ("roff", 8), ("loff", 48)):
+        s[name] = ("sbuf", [128, cols], "uint16")
+    pairs = [("uq", "us", 176), ("sq", "ss", 448), ("zq", "zs", 128), ("cq", "cs", 128), ("lq", "ls", 256),
+             ("eq", "es", 512), ("fq", "fs", 512), ("bq", "bs", 128)]
+    pairs += [("xq%d" % t, "xs%d" % t, 258) for t in range(R + 1)]
+    pairs += [("%sq%d" % (n, t), "%ss%d" % (n, t), 256) for t in range(R) for n in ("la", "ro", "vv", "vp")]
+    for q, p, cols in pairs:
+        s[q] = ("sbuf", [128, cols], Q8)
+        s[p] = ("sbuf", [128, cols], "uint8")
+    s["pa"] = ("psum", [128, 2048], "float32")
+    s["pb"] = ("psum", [128, 2048], "float32")
+    return s
+
+
+SCRATCH = _scratch()
+SEMAPHORES = (["sv", "sa", "sp", "sg", "lw", "lxa", "lxb", "lz", "sto", "sent"]
+              + ["arrc%d" % t for t in range(R)] + ["arrs%d" % t for t in range(R)])
+
+
+def rank_program(g, core, T, topo):
+    rank = T.rank_of(core)
+    if rank is None:
+        return
+    A = AluOpType
+    F = ActivationFunctionType
+    cores = list(T.cores)
+    n = len(cores)
+    queues = {"V": g.vector, "S": g.scalar, "P": g.tensor, "G": g, "Y": g.sync}
+    count = {}
+    waited = {q: {} for q in queues}
+
+    def wait(q, *deps):
+        need = {}
+        for d in deps:
+            if d is not None:
+                need[d[0]] = max(need.get(d[0], 0), d[1])
+        for s, c in need.items():
+            if waited[q].get(s, 0) < c:
+                queues[q].wait_ge(T.sem[s], c)
+                waited[q][s] = c
+
+    def done(ins, s, k=1):
+        ins.then_inc(T.sem[s], k)
+        count[s] = count.get(s, 0) + k
+        return (s, count[s])
+
+    def ts(out, in0, s1, s2, op0, op1=None, deps=()):
+        wait("V", *deps)
+        if op1 is None:
+            return done(g.vector.tensor_scalar(out, in0, s1, None, op0), "sv")
+        return done(g.vector.tensor_scalar(out, in0, s1, s2, op0, op1), "sv")
+
+    def tt(out, in0, in1, op, deps=()):
+        wait("V", *deps)
+        return done(g.vector.tensor_tensor(out, in0, in1, op), "sv")
+
+    def cp(out, in_, deps=()):
+        wait("V", *deps)
+        return done(g.vector.tensor_copy(out, in_), "sv")
+
+    def ms(out, c, deps=()):
+        wait("V", *deps)
+        return done(g.vector.memset(out, c), "sv")
+
+    def red(out, in_, op, deps=()):
+        wait("V", *deps)
+        return done(g.vector.tensor_reduce(out, in_, AxisListType.X, op), "sv")
+
+    def scan(out, d0, d1, init, op0, op1, deps=()):
+        wait("V", *deps)
+        return done(g.vector.tensor_tensor_scan(out, d0, d1, init, op0, op1), "sv")
+
+    def qz(q, s, in_, deps=()):
+        wait("V", *deps)
+        return done(g.vector.quantize_mx(q, s, in_), "sv")
+
+    def act(out, in_, func, deps=(), **kw):
+        wait("S", *deps)
+        return done(g.scalar.activation(out, in_, func, **kw), "sa")
+
+    def mm(out, lq, ls, a, rq, rs, b, w, start, stop, deps=()):
+        wait("P", *deps)
+        return done(g.tensor.matmul_mx(out, lq[:, a:a + 128], ls[:, a:a + 128], rq[:, b:b + w], rs[:, b:b + w],
+                                       start, stop), "sp")
+
+    def iota(out, pattern, base, cm, small):
+        if small:
+            return done(g.iota(out, pattern, base, cm, allow_small_or_imprecise_dtypes=True), "sg")
+        return done(g.iota(out, pattern, base, cm), "sg")
+
+    def dma(q, out, in_, s, deps=()):
+        wait(q, *deps)
+        return done(queues[q].dma_start(out, in_), s, 16)
+
+    def pickq(out, win, off, deps):
+        return cp(out.bitcast(dt.uint32), win.bitcast(dt.uint32).indirect(off), deps)
+
+    def picks(out, win, off, deps):
+        return act(out, win.indirect(off), F.Copy, deps)
+
+    def bank(buf, b, w):
+        return buf[:, 512 * b:512 * b + w]
+
+    others = [cores[(rank + k) % n] for k in range(1, n)]
+    mask = topo.mask(core, others[0])
+    for o in others[1:]:
+        mask = mask & topo.mask(core, o)
+    lanes = bin(mask).count("1")
+    ids = [DstId(rid=topo.addr(o)[0], pnc=topo.addr(o)[1]) for o in others]
+
+    def spread(view, sem, deps):
+        wait("G", *deps)
+        tr = RemoteDMATransfer(dst_ids=ids, dma_engine_mask=mask, remote_sem=T.sem[sem],
+                               srcs=[view()], dsts=[view() for o in others])
+        g.remote_dma_fused([tr], local_sem=T.sem.sent)
+        count["sent"] = count.get("sent", 0) + lanes
+        return (sem, lanes * (n - 1))
+
+    BIT = 2.0 ** 27
+    DOWN = 2.0 ** -44
+
+    t_xa = dma("S", T.xin[:, 0:512], T.x[:, 0:512], "lxa")
+    t_w = dma("Y", T.ut[:, 128:224], T.w[:, 0:96], "lw")
+    t_xb = dma("Y", T.xin[:, 512:1024], T.x[:, 512:1024], "lxb")
+    t_z = dma("Y", T.zin[:], T.z[:], "lz", [t_xb])
+
+    i_v0 = iota(T.vi[32:64, 0:6], [[1, 6]], 0, -1, True)
+    i_v1 = iota(T.vi[0:32, 0:6], [[1, 6]], 0, -1, True)
+    wait("G", i_v0)
+    i_l = iota(T.li[0:64, :], [[16, 2], [0, 2], [1, 16]], 0, 0, True)
+    i_vb = iota(T.vb[:], [[1, 128]], 128, -1, False)
+    i_p = iota(T.pint[:, 0:1], [[0, 1]], 0, 1, False)
+    i_k = iota(T.k2[:], [[2, 16]], 0, 0, True)
+
+    t_zz = ms(T.zz[:], 0.0)
+    ms(T.ut[:, 0:128], 0.0)
+    t_ut = ms(T.ut[:, 224:704], 0.0)
+    t_ct = ms(T.ct[:], 0.0)
+    s_z0 = act(T.st[:, 0:256], T.zz[:], F.Copy, [t_zz])
+    s_z1 = act(T.st[:, 512:768], T.zz[:], F.Copy)
+    act(T.cl[:, 0:256], T.zz[:], F.Copy)
+    act(T.cl[:, 256:512], T.zz[:], F.Copy)
+    a0 = ts(T.fa[0:64, 0:5], T.vi[0:64, 0:5], 1.0, 0.5, A.min, A.max, [i_v1])
+    a1 = ts(T.fa[0:64, 5:6], T.vi[0:64, 5:6], 1.0, 0.0, A.min, A.max)
+    ms(T.bt[:, 1:512:4], BIT)
+    a2 = red(T.sca[0:64, 0:1], T.fa[0:64, 0:6], A.mult, [a0, a1])
+    ms(T.bt[:, 2:512:4], 0.0)
+    a3 = ts(T.yb[0:64, :], T.li[0:64, :], 0.5, T.sca[0:64, 0:1], A.add, A.mult, [a2, i_l])
+    t_bt = ms(T.bt[:, 3:512:4], 0.0)
+    a4 = cp(T.yi[0:64, :], T.yb[0:64, :], [a3])
+    t_xt = ms(T.xin[:, 1024:1032], 0.0)
+    a5 = tt(T.db[0:64, :], T.yi[0:64, :], T.yb[0:64, :], A.subtract, [a4])
+    ms(T.score[0:64, 128:129], -(2.0 ** 30))
+    t_sc = ms(T.score[64:128, 128:129], -(2.0 ** 26))
+    c0 = act(T.ct[0:32, 0:256:4], T.db[0:32, :], F.Sign, [a5, t_ct])
+    c1 = act(T.ct[32:64, 256:512:4], T.db[32:64, :], F.Sign)
+    act(T.cl[:, 512:768], T.zz[:], F.Copy)
+    s_cl = act(T.cl[:, 768:1024], T.zz[:], F.Copy)
+    c2 = ts(T.ct[0:32, 1:256:4], T.db[0:32, :], 0.0, -1.0, A.is_gt, A.mult, [a5, t_ct])
+    c3 = ts(T.ct[32:64, 257:512:4], T.db[32:64, :], 0.0, -1.0, A.is_gt, A.mult)
+    t_fe0 = ms(T.fe[:], 0.0)
+    t_cq = qz(T.cq[:], T.cs[:], T.ct[:], [c0, c1, c2, c3])
+    t_fe = ts(T.fe[:, 3:515:4], T.vb[:], 128.0, 0.125, A.is_equal, A.mult, [t_fe0, i_vb])
+    r0 = ms(T.rm8[:], 1.0)
+    r1 = ms(T.rm16[:], 1.0)
+    t_ht = ms(T.ht[:, 1024:1032], 0.0)
+    t_rm8 = ms(T.rm8[:, 0:256:8], 0.0, [r0])
+    t_rm16 = ms(T.rm16[:, 0:256:16], 0.0, [r1])
+
+    def repeat(t):
+        tok = None
+        for e in range(4):
+            lo = 4 * (64 + 128 * t)
+            col = 128 + 4 * (8 * t + 6) + e
+            tok = act(T.st[:, lo + e:lo + 256:4], T.zz[:, 0:64], F.Identity, [t_w], bias=T.ut[:, col:col + 1])
+        return tok
+
+    s_r0 = repeat(0)
+    s_ff = act(T.ff[:], T.fe[:], F.Copy, [t_fe], scale=-0.5)
+    t_uq = qz(T.uq[:], T.us[:], T.ut[:], [t_w, t_ut])
+    x_a = qz(T.xq0[:, 0:128], T.xs0[:, 0:128], T.xin[:, 0:512], [t_xa])
+    x_b = qz(T.xq0[:, 128:258], T.xs0[:, 128:258], T.xin[:, 512:1032], [t_xb, t_xt])
+    t_sq = qz(T.sq[:, 0:192], T.ss[:, 0:192], T.st[:, 0:768], [s_r0, s_z0, s_z1])
+
+    late = {}
+    for t in range(R):
+        xq, xs = T["xq%d" % t], T["xs%d" % t]
+        laq, las = T["laq%d" % t], T["las%d" % t]
+        roq, ros = T["roq%d" % t], T["ros%d" % t]
+        vvq, vvs = T["vvq%d" % t], T["vvs%d" % t]
+        vpq, vps = T["vpq%d" % t], T["vps%d" % t]
+        nq, ns = T["xq%d" % (t + 1)], T["xs%d" % (t + 1)]
+
+        mm(bank(T.pb, 0, 128), T.uq, T.us, 32 + 8 * t, xq, xs, 0, 128, True, False, [t_uq, x_a])
+        p_pl = mm(bank(T.pb, 0, 128), T.uq, T.us, 8 * t, xq, xs, 128, 128, False, True, [x_b])
+        mm(bank(T.pb, 1, 128), T.sq, T.ss, 64 + 128 * t, xq, xs, 0, 128, True, False, [t_sq])
+        p_st = mm(bank(T.pb, 1, 128), T.sq, T.ss, 128 * t, xq, xs, 128, 128, False, True)
+        v_lt = ts(T.bt[:, 0:512:4], bank(T.pb, 0, 128), 0.0, BIT, A.is_lt, A.mult, [p_pl])
+        v_bq = qz(T.bq[:], T.bs[:], T.bt[:], [v_lt, t_bt])
+        s_ss = act(T.ssc[:], bank(T.pb, 1, 128), F.Copy, [p_st], scale=DOWN)
+        p_pen = mm(bank(T.pb, 2, 128), T.cq, T.cs, 0, T.bq, T.bs, 0, 128, True, True, [v_bq, t_cq])
+        v_add = tt(T.score[:, 0:128], bank(T.pb, 2, 128), T.ssc[:], A.add, [p_pen, s_ss])
+        v_pm = scan(T.pm[:, 0:129], T.score[:, 0:129], T.score[:, 0:129], -(2.0 ** 31), A.max, A.max, [v_add, t_sc])
+        s_cnt = act(T.junk[:, 0:129], T.pm[:, 0:129], F.Sign, [v_pm], bias=T.pm[:, 128:129], scale=-1.0,
+                    accum_out=T.cnt[:, 0:1])
+        v_g1 = ts(T.g1[0:64, 0:1], T.pm[64:128, 128:129], T.pm[0:64, 128:129], 512.0, A.is_gt, A.mult, [v_pm])
+        v_g2 = ts(T.g2[0:64, 0:1], T.g1[0:64, 0:1], -384.0, None, A.add, None, [v_g1])
+        rs = []
+        for qd in range(2):
+            for k in range(2):
+                rs.append(ts(T.roff[32 * qd:32 * qd + 32, 2 * t + k:2 * t + k + 1], T.cnt[64 + 32 * k:96 + 32 * k, 0:1],
+                             T.g2[32 * k:32 * k + 32, 0:1], T.cnt[32 * k:32 * k + 32, 0:1], A.add, A.max,
+                             [v_g2, s_cnt]))
+        v_ro = cp(T.roff[64:128, 2 * t:2 * t + 2], T.roff[0:64, 2 * t:2 * t + 2], rs)
+        lo, hi = NL * rank, NL * rank + NL
+        v_pk = pickq(laq[:, lo:hi], xq[:, 0:258], T.roff[:, 2 * t:2 * t + 2], [v_ro])
+        s_pk = picks(las[:, lo:hi], xs[:, 0:258], T.roff[:, 2 * t:2 * t + 2], [v_ro])
+
+        a_c = spread(lambda: laq[:, lo:hi].bitcast(dt.uint8), "arrc%d" % t, [v_pk])
+        a_s = spread(lambda: las[:, lo:hi], "arrs%d" % t, [s_pk])
+
+        if t == 0:
+            b0 = ts(T.fb[0:64, 0:4], T.vi[0:64, 0:4], 0.0, 1.0, A.is_lt, A.add)
+            b1 = ts(T.fb[0:64, 4:5], T.vi[0:64, 5:6], 1.0, 0.0, A.min, A.max)
+            k0 = ts(T.pa7[:, 0:1], T.pint[:, 0:1], 7, None, A.bitwise_and, None, [i_p, i_k])
+            k1 = ts(T.pb1[:, 0:1], T.pint[:, 0:1], 3, 1, A.logical_shift_right, A.bitwise_and)
+            b2 = red(T.scb[0:64, 0:1], T.fb[0:64, 0:5], A.mult, [b0, b1])
+            k2 = ts(T.pf[:, 0:1], T.pa7[:, 0:1], 32.0, None, A.mult, None, [k0])
+            k3 = cp(T.pf[:, 1:2], T.pb1[:, 0:1], [k1])
+            b3 = ts(T.cl[0:32, 0:512:4], T.zz[0:32, 0:128], T.scb[0:32, 0:1], 1.0 / BIT, A.add, A.mult, [b2, s_cl])
+            b4 = ts(T.cl[32:64, 512:1024:4], T.zz[32:64, 0:128], T.scb[32:64, 0:1], 1.0 / BIT, A.add, A.mult)
+            late["coff"] = ts(T.coff[:], T.k2[:], T.pf[:, 0:1], T.pf[:, 1:2], A.add, A.add, [k2, k3])
+            late["lq"] = qz(T.lq[:], T.ls[:], T.cl[:], [b3, b4])
+            e0 = ts(T.vm[:], T.vb[:], 15, None, A.bitwise_and)
+            for b in range(4):
+                late["eq"] = qz(T.eq[:, 128 * b:128 * b + 128], T.es[:, 128 * b:128 * b + 128],
+                                T.fe[:, 3 - b:515 - b], [t_fe])
+            late["sel"] = ts(T.sel[:], T.vm[:], 0.0, None, A.is_equal, None, [e0])
+            act(T.st[:, 1024:1280], T.zz[:], F.Copy)
+            act(T.st[:, 1536:1792], T.zz[:], F.Copy)
+            repeat(1)
+            late["st"] = repeat(2)
+        p_la = mm(bank(T.pb, 3, 128), T.lq, T.ls, 0, T.bq, T.bs, 0, 128, True, True, [late["lq"]])
+        p_lb = mm(bank(T.pb, 0, 128), T.lq, T.ls, 128, T.bq, T.bs, 0, 128, True, True)
+        for b in range(4):
+            mm(bank(T.pa, b, 256), T.eq, T.es, 128 * b, xq, xs, 0, 256, True, False, [late["eq"]])
+        s_la = act(T.lrow[:, 256 * t:256 * t + 128], bank(T.pb, 3, 128), F.Copy, [p_la])
+        s_lb = act(T.lrow[:, 256 * t + 128:256 * t + 256], bank(T.pb, 0, 128), F.Copy, [p_lb])
+        if t == 0:
+            for b in range(4):
+                late["fq"] = qz(T.fq[:, 128 * b:128 * b + 128], T.fs[:, 128 * b:128 * b + 128],
+                                T.ff[:, 3 - b:515 - b], [s_ff])
+        l0 = tt(T.lm[:, 0:128], bank(T.pb, 3, 128), T.sel[:], A.mult, [s_la, late["sel"]])
+        l1 = tt(T.lm[:, 128:256], bank(T.pb, 0, 128), T.sel[:], A.mult, [s_lb])
+        l2 = scan(T.lsc[:], T.rm16[:], T.lm[:], 0.0, A.mult, A.add, [l0, l1, t_rm16])
+        off = T.loff[:, 16 * t:16 * t + 16]
+        v_lo = ts(off, T.lsc[:, 15:256:16], 8.0, 7.0, A.mult, A.add, [l2])
+        if t == 0:
+            t_sq = qz(T.sq[:, 192:448], T.ss[:, 192:448], T.st[:, 768:1792], [late["st"]])
+        if t == 1:
+            late["zq"] = qz(T.zq[:], T.zs[:], T.zin[:], [t_z])
+        if t == R - 1:
+            dma("Y", T.lv[:], T.lrow[0:1, 0:768], "sto", [s_lb])
+
+        v_or = pickq(roq[:], laq[:], T.coff[:], [a_c, late["coff"], v_pk])
+        s_or = picks(ros[:], las[:], T.coff[:], [a_s, late["coff"], s_pk])
+        sums = []
+        for b in range(4):
+            p_d = mm(bank(T.pb, b, 256), T.eq, T.es, 128 * b, roq, ros, 0, 256, True, True, [v_or, s_or])
+            sums.append(scan(T.vt[:, b:1024:4], T.rm8[:], bank(T.pb, b, 256), 0.0, A.mult, A.add, [p_d, t_rm8]))
+        v_vq = qz(vvq[:], vvs[:], T.vt[:], sums)
+
+        v_vp = pickq(vpq[:], vvq[:], T.loff[:, 16 * t:16 * t + 16], [v_vq, v_lo])
+        s_vp = picks(vps[:], vvs[:], T.loff[:, 16 * t:16 * t + 16], [v_vq, v_lo])
+        outs = []
+        for b in range(4):
+            p_s = mm(bank(T.pa, b, 256), T.fq, T.fs, 128 * b, vpq, vps, 0, 256, False, True, [v_vp, s_vp, late["fq"]])
+            if b % 2 == 0:
+                outs.append(act(T.ht[:, b:1024:4], bank(T.pa, b, 256), F.Copy, [p_s], scale=8.0))
+            else:
+                outs.append(ts(T.ht[:, b:1024:4], bank(T.pa, b, 256), 8.0, None, A.mult, None, [p_s]))
+        x_a = qz(nq[:, 0:128], ns[:, 0:128], T.ht[:, 0:512], outs)
+        x_b = qz(nq[:, 128:258], ns[:, 128:258], T.ht[:, 512:1032], [t_ht])
+
+    xq, xs = T["xq%d" % R], T["xs%d" % R]
+    p_ya = mm(bank(T.pb, 0, 128), T.zq, T.zs, 0, xq, xs, 0, 128, True, True, [x_a, late["zq"]])
+    p_yb = mm(bank(T.pb, 1, 128), T.zq, T.zs, 0, xq, xs, 128, 128, True, True, [x_b])
+    dma("Y", T.oc[:, 0:4 * TC], xq[:, 0:TC].bitcast(dt.uint8), "sto", [x_b])
+    for k in range(4):
+        dma("Y" if k < 2 else "S", T.osc[4 * k:4 * k + 4, 0:TC], xs[32 * k:32 * k + 4, 0:TC], "sto", [x_b])
+    v_ya = cp(T.yo[:, 0:128], bank(T.pb, 0, 128), [p_ya])
+    v_yb = cp(T.yo[:, 128:256], bank(T.pb, 1, 128), [p_yb])
+    dma("Y", T.y[:, 0:128], T.yo[:, 0:128], "sto", [v_ya])
+    dma("S", T.y[:, 128:256], T.yo[:, 128:256], "sto", [v_yb])
+    wait("G", *[(s, count[s]) for s in ("sent", "sg", "sp", "sa", "sv")])
+    wait("Y", ("sto", count["sto"]))

@@ -17,21 +17,20 @@ def _scratch():
                        ("ct", 512),
                        ("cl", 1024),
                        ("fe", 520),
-                       ("ff", 520),
-                       ("rm8", 256), ("rm16", 256),
+                       ("rm8", 256), ("vb", 128),
                        ("bt", 512),
                        ("vt", 1024)):
         s[name] = ("sbuf", [128, cols], "bfloat16")
-    for name, cols in (("vi", 8), ("li", 64), ("fa", 8), ("fb", 8), ("sca", 4), ("scb", 4), ("yb", 64), ("db", 64),
-                       ("sel", 128), ("pf", 4), ("k2", 16), ("ssc", 128), ("score", 132), ("pm", 132), ("junk", 132),
-                       ("cnt", 4), ("g1", 4), ("g2", 4), ("lrow", 768), ("lm", 256), ("lsc", 256), ("yo", 256)):
+    for name, cols in (("vi", 8), ("li", 64), ("fa", 8), ("fb", 8), ("sca", 4), ("scb", 4), ("m16", 128),
+                       ("pf", 4), ("k2", 16), ("pm", 132), ("junk", 132),
+                       ("cnt", 4), ("g1", 4), ("g2", 4), ("lrow", 768), ("lsc", 256), ("yo", 256)):
         s[name] = ("sbuf", [128, cols], "float32")
-    for name, cols in (("yi", 64), ("vb", 128), ("vm", 128), ("pint", 4), ("pa7", 4), ("pb1", 4)):
+    for name, cols in (("yi", 64), ("yb", 64), ("pint", 4), ("pa7", 4)):
         s[name] = ("sbuf", [128, cols], "int32")
     for name, cols in (("coff", 16), ("roff", 8), ("loff", 48)):
         s[name] = ("sbuf", [128, cols], "uint16")
     pairs = [("uq", "us", 176), ("sq", "ss", 448), ("zq", "zs", 128), ("cq", "cs", 128), ("lq", "ls", 256),
-             ("eq", "es", 512), ("fq", "fs", 512), ("bq", "bs", 128)]
+             ("eq", "es", 512), ("bq", "bs", 128)]
     pairs += [("xq%d" % t, "xs%d" % t, 258) for t in range(R + 1)]
     pairs += [("%sq%d" % (n, t), "%ss%d" % (n, t), 256) for t in range(R) for n in ("la", "ro", "vv", "vp")]
     for q, p, cols in pairs:
@@ -80,10 +79,6 @@ def rank_program(g, core, T, topo):
             return done(g.vector.tensor_scalar(out, in0, s1, None, op0), "sv")
         return done(g.vector.tensor_scalar(out, in0, s1, s2, op0, op1), "sv")
 
-    def tt(out, in0, in1, op, deps=()):
-        wait("V", *deps)
-        return done(g.vector.tensor_tensor(out, in0, in1, op), "sv")
-
     def cp(out, in_, deps=()):
         wait("V", *deps)
         return done(g.vector.tensor_copy(out, in_), "sv")
@@ -113,7 +108,8 @@ def rank_program(g, core, T, topo):
         return done(g.tensor.matmul_mx(out, lq[:, a:a + 128], ls[:, a:a + 128], rq[:, b:b + w], rs[:, b:b + w],
                                        start, stop), "sp")
 
-    def iota(out, pattern, base, cm, small):
+    def iota(out, pattern, base, cm, small, deps=()):
+        wait("G", *deps)
         if small:
             return done(g.iota(out, pattern, base, cm, allow_small_or_imprecise_dtypes=True), "sg")
         return done(g.iota(out, pattern, base, cm), "sg")
@@ -122,10 +118,10 @@ def rank_program(g, core, T, topo):
         wait(q, *deps)
         return done(queues[q].dma_start(out, in_), s, 16)
 
-    def pickq(out, win, off, deps):
+    def pickq(out, win, off, deps=()):
         return cp(out.bitcast(dt.uint32), win.bitcast(dt.uint32).indirect(off), deps)
 
-    def picks(out, win, off, deps):
+    def picks(out, win, off, deps=()):
         return act(out, win.indirect(off), F.Copy, deps)
 
     def bank(buf, b, w):
@@ -146,56 +142,58 @@ def rank_program(g, core, T, topo):
         count["sent"] = count.get("sent", 0) + lanes
         return (sem, lanes * (n - 1))
 
-    BIT = 2.0 ** 27
-    DOWN = 2.0 ** -44
+    BIT = 2.0 ** 30
+    PEN = 2.0 ** 42
+    LOW = -(2.0 ** 70)
+    UNP = -0.0625
 
-    t_xa = dma("S", T.xin[:, 0:512], T.x[:, 0:512], "lxa")
+    t_xa = dma("S", T.xin[:, 8:520], T.x[:, 0:512], "lxa")
     t_w = dma("Y", T.ut[:, 128:224], T.w[:, 0:96], "lw")
-    t_xb = dma("Y", T.xin[:, 512:1024], T.x[:, 512:1024], "lxb")
+    t_xb = dma("Y", T.xin[:, 520:1032], T.x[:, 512:1024], "lxb")
     t_z = dma("Y", T.zin[:], T.z[:], "lz", [t_xb])
 
-    i_v0 = iota(T.vi[32:64, 0:6], [[1, 6]], 0, -1, True)
-    i_v1 = iota(T.vi[0:32, 0:6], [[1, 6]], 0, -1, True)
-    wait("G", i_v0)
-    i_l = iota(T.li[0:64, :], [[16, 2], [0, 2], [1, 16]], 0, 0, True)
-    i_vb = iota(T.vb[:], [[1, 128]], 128, -1, False)
-    i_p = iota(T.pint[:, 0:1], [[0, 1]], 0, 1, False)
-    i_k = iota(T.k2[:], [[2, 16]], 0, 0, True)
+    i_v0 = iota(T.vi[32:64, 0:4], [[1, 4]], 2, -1, True)
+    i_v = iota(T.vi[0:32, 0:4], [[1, 4]], 2, -1, True)
+    i_l = iota(T.li[0:64, :], [[16, 2], [0, 2], [1, 16]], 0, 0, True, [i_v0])
 
     t_zz = ms(T.zz[:], 0.0)
+    t_b1 = ms(T.bt[:, 1:512:4], BIT)
+    ms(T.bt[96:128, 0:512:4], 0.0)
     ms(T.ut[:, 0:128], 0.0)
     t_ut = ms(T.ut[:, 224:704], 0.0)
     t_ct = ms(T.ct[:], 0.0)
+    wait("G", t_b1, i_l)
+    i_sel = done(g.affine_select(T.bt[64:96, 0:512:4], T.bt[64:96, 1:512:4], [[0, 8], [1, 16]], A.is_equal, 0.0, 0, -1),
+                 "sg")
+    i_vb = iota(T.vb[:], [[1, 128]], 0, -1, True, [i_sel])
+    iota(T.pint[:, 0:1], [[0, 1]], 0, 257, False)
+    i_m = iota(T.m16[:], [[0, 8], [100, 16]], 0, 0, True)
+    i_k = iota(T.k2[:], [[2, 16]], 0, 0, True)
+    for qd in (1, 3):
+        i_k = iota(T.k2[32 * qd:32 * qd + 32, :], [[-16, 2], [2, 8]], 16, 0, True, [i_k])
+
     s_z0 = act(T.st[:, 0:256], T.zz[:], F.Copy, [t_zz])
     s_z1 = act(T.st[:, 512:768], T.zz[:], F.Copy)
-    act(T.cl[:, 0:256], T.zz[:], F.Copy)
-    act(T.cl[:, 256:512], T.zz[:], F.Copy)
-    a0 = ts(T.fa[0:64, 0:5], T.vi[0:64, 0:5], 1.0, 0.5, A.min, A.max, [i_v1])
-    a1 = ts(T.fa[0:64, 5:6], T.vi[0:64, 5:6], 1.0, 0.0, A.min, A.max)
-    ms(T.bt[:, 1:512:4], BIT)
-    a2 = red(T.sca[0:64, 0:1], T.fa[0:64, 0:6], A.mult, [a0, a1])
-    ms(T.bt[:, 2:512:4], 0.0)
-    a3 = ts(T.yb[0:64, :], T.li[0:64, :], 0.5, T.sca[0:64, 0:1], A.add, A.mult, [a2, i_l])
-    t_bt = ms(T.bt[:, 3:512:4], 0.0)
-    a4 = cp(T.yi[0:64, :], T.yb[0:64, :], [a3])
-    t_xt = ms(T.xin[:, 1024:1032], 0.0)
-    a5 = tt(T.db[0:64, :], T.yi[0:64, :], T.yb[0:64, :], A.subtract, [a4])
-    ms(T.score[0:64, 128:129], -(2.0 ** 30))
-    t_sc = ms(T.score[64:128, 128:129], -(2.0 ** 26))
-    c0 = act(T.ct[0:32, 0:256:4], T.db[0:32, :], F.Sign, [a5, t_ct])
-    c1 = act(T.ct[32:64, 256:512:4], T.db[32:64, :], F.Sign)
-    act(T.cl[:, 512:768], T.zz[:], F.Copy)
-    s_cl = act(T.cl[:, 768:1024], T.zz[:], F.Copy)
-    c2 = ts(T.ct[0:32, 1:256:4], T.db[0:32, :], 0.0, -1.0, A.is_gt, A.mult, [a5, t_ct])
-    c3 = ts(T.ct[32:64, 257:512:4], T.db[32:64, :], 0.0, -1.0, A.is_gt, A.mult)
-    t_fe0 = ms(T.fe[:], 0.0)
-    t_cq = qz(T.cq[:], T.cs[:], T.ct[:], [c0, c1, c2, c3])
-    t_fe = ts(T.fe[:, 3:515:4], T.vb[:], 128.0, 0.125, A.is_equal, A.mult, [t_fe0, i_vb])
-    r0 = ms(T.rm8[:], 1.0)
-    r1 = ms(T.rm16[:], 1.0)
-    t_ht = ms(T.ht[:, 1024:1032], 0.0)
-    t_rm8 = ms(T.rm8[:, 0:256:8], 0.0, [r0])
-    t_rm16 = ms(T.rm16[:, 0:256:16], 0.0, [r1])
+    act(T.bt[:, 2:512:4], T.zz[:, 0:128], F.Copy)
+    s_bt = act(T.bt[:, 3:512:4], T.zz[:, 0:128], F.Copy)
+    a0 = ts(T.fa[0:64, 0:4], T.vi[0:64, 0:4], 2.0, 1.0, A.min, A.max, [i_v])
+    a1 = ts(T.fa[0:64, 4:5], T.vi[0:64, 3:4], 1.0, PEN / 8, A.is_ge, A.mult)
+    t_xt = ms(T.xin[:, 0:8], 0.0)
+    a2 = red(T.sca[0:64, 0:1], T.fa[0:64, 0:5], A.mult, [a0, a1])
+    t_pm = ms(T.pm[:, 0:2], LOW)
+    a3 = ts(T.yi[0:64, :], T.li[0:64, :], T.sca[0:64, 0:1], 8 / PEN, A.mult, A.mult, [a2, i_l])
+    t_ht = ms(T.ht[:, 0:8], 0.0)
+    a4 = ts(T.yb[0:64, :], T.yi[0:64, :], 16, None, A.bitwise_and, None, [a3])
+    b0 = ts(T.fb[0:64, 0:4], T.vi[0:64, 0:4], 2.0, 1.0, A.is_lt, A.add)
+    cs = []
+    for h in range(2):
+        lo = 32 * h
+        cs.append(ts(T.ct[lo:lo + 32, 256 * h:256 * h + 256:4], T.yb[lo:lo + 32, :], -8.0, T.fa[lo:lo + 32, 4:5],
+                     A.add, A.mult, [a4, t_ct]))
+        cs.append(ts(T.ct[lo:lo + 32, 256 * h + 1:256 * h + 256:4], T.yb[lo:lo + 32, :], -PEN / 16, None, A.mult))
+    b1 = ts(T.fb[0:64, 4:5], T.vi[0:64, 3:4], 1.0, 1.0 / (BIT * BIT), A.is_ge, A.mult)
+    t_cq = qz(T.cq[:], T.cs[:], T.ct[:], cs)
+    b2 = red(T.scb[0:64, 0:1], T.fb[0:64, 0:5], A.mult, [b0, b1])
 
     def repeat(t):
         tok = None
@@ -206,11 +204,13 @@ def rank_program(g, core, T, topo):
         return tok
 
     s_r0 = repeat(0)
-    s_ff = act(T.ff[:], T.fe[:], F.Copy, [t_fe], scale=-0.5)
+    s_cl = None
+    for k in range(4):
+        s_cl = act(T.cl[:, 256 * k:256 * k + 256], T.zz[:], F.Copy)
     t_uq = qz(T.uq[:], T.us[:], T.ut[:], [t_w, t_ut])
-    x_a = qz(T.xq0[:, 0:128], T.xs0[:, 0:128], T.xin[:, 0:512], [t_xa])
-    x_b = qz(T.xq0[:, 128:258], T.xs0[:, 128:258], T.xin[:, 512:1032], [t_xb, t_xt])
+    x_a = qz(T.xq0[:, 0:130], T.xs0[:, 0:130], T.xin[:, 0:520], [t_xa, t_xt])
     t_sq = qz(T.sq[:, 0:192], T.ss[:, 0:192], T.st[:, 0:768], [s_r0, s_z0, s_z1])
+    x_b = qz(T.xq0[:, 130:258], T.xs0[:, 130:258], T.xin[:, 520:1032], [t_xb])
 
     late = {}
     for t in range(R):
@@ -221,27 +221,38 @@ def rank_program(g, core, T, topo):
         vpq, vps = T["vpq%d" % t], T["vps%d" % t]
         nq, ns = T["xq%d" % (t + 1)], T["xs%d" % (t + 1)]
 
-        mm(bank(T.pb, 0, 128), T.uq, T.us, 32 + 8 * t, xq, xs, 0, 128, True, False, [t_uq, x_a])
-        p_pl = mm(bank(T.pb, 0, 128), T.uq, T.us, 8 * t, xq, xs, 128, 128, False, True, [x_b])
-        mm(bank(T.pb, 1, 128), T.sq, T.ss, 64 + 128 * t, xq, xs, 0, 128, True, False, [t_sq])
-        p_st = mm(bank(T.pb, 1, 128), T.sq, T.ss, 128 * t, xq, xs, 128, 128, False, True)
-        v_lt = ts(T.bt[:, 0:512:4], bank(T.pb, 0, 128), 0.0, BIT, A.is_lt, A.mult, [p_pl])
-        v_bq = qz(T.bq[:], T.bs[:], T.bt[:], [v_lt, t_bt])
-        s_ss = act(T.ssc[:], bank(T.pb, 1, 128), F.Copy, [p_st], scale=DOWN)
-        p_pen = mm(bank(T.pb, 2, 128), T.cq, T.cs, 0, T.bq, T.bs, 0, 128, True, True, [v_bq, t_cq])
-        v_add = tt(T.score[:, 0:128], bank(T.pb, 2, 128), T.ssc[:], A.add, [p_pen, s_ss])
-        v_pm = scan(T.pm[:, 0:129], T.score[:, 0:129], T.score[:, 0:129], -(2.0 ** 31), A.max, A.max, [v_add, t_sc])
-        s_cnt = act(T.junk[:, 0:129], T.pm[:, 0:129], F.Sign, [v_pm], bias=T.pm[:, 128:129], scale=-1.0,
+        mm(bank(T.pa, 0, 128), T.uq, T.us, 32 + 8 * t, xq, xs, 2, 128, True, False, [t_uq, x_a])
+        mm(bank(T.pa, 1, 128), T.sq, T.ss, 64 + 128 * t, xq, xs, 2, 128, True, False, [t_sq])
+        p_pl = mm(bank(T.pa, 0, 128), T.uq, T.us, 8 * t, xq, xs, 130, 128, False, True, [x_b])
+        mm(bank(T.pa, 1, 128), T.sq, T.ss, 128 * t, xq, xs, 130, 128, False, False)
+        if t == 0:
+            t_fe0 = ms(T.fe[:], 0.0)
+        v_lt = ts(T.bt[0:64, 0:512:4], T.pa[0:64, 0:128], 0.0, BIT, A.is_lt, A.mult, [p_pl])
+        v_bq = qz(T.bq[:], T.bs[:], T.bt[:], [v_lt, s_bt, i_sel])
+        p_pen = mm(bank(T.pa, 1, 128), T.cq, T.cs, 0, T.bq, T.bs, 0, 128, False, True, [v_bq, t_cq])
+        if t == 0:
+            t_fe = ts(T.fe[:, 3:515:4], T.vb[:], 0.0, UNP, A.is_equal, A.mult, [t_fe0, i_vb])
+            r0 = ms(T.rm8[:], 1.0)
+            lc = []
+            for h in range(2):
+                lo = 32 * h
+                lc.append(act(T.cl[lo:lo + 32, 512 * h:512 * h + 512:4], T.bt[lo:lo + 32, 1:512:4], F.Identity,
+                              [s_cl, b2], scale=T.scb[lo:lo + 32, 0:1]))
+                lc.append(act(T.cl[64:96, 512 * h:512 * h + 512:4], T.bt[64:96, 0:512:4], F.Copy, [i_sel],
+                              scale=64.0 / (BIT * BIT)))
+        v_pm = scan(T.pm[:, 2:130], bank(T.pa, 1, 128), T.zz[:, 0:128], LOW, A.max, A.add, [p_pen, t_pm])
+        s_cnt = act(T.junk[:, 0:130], T.pm[:, 0:130], F.Sign, [v_pm], bias=T.pm[:, 129:130], scale=-1.0,
                     accum_out=T.cnt[:, 0:1])
-        v_g1 = ts(T.g1[0:64, 0:1], T.pm[64:128, 128:129], T.pm[0:64, 128:129], 512.0, A.is_gt, A.mult, [v_pm])
+        v_g1 = ts(T.g1[0:64, 0:1], T.pm[64:128, 129:130], T.pm[0:64, 129:130], 512.0, A.is_gt, A.mult, [v_pm])
         v_g2 = ts(T.g2[0:64, 0:1], T.g1[0:64, 0:1], -384.0, None, A.add, None, [v_g1])
-        rs = []
-        for qd in range(2):
-            for k in range(2):
-                rs.append(ts(T.roff[32 * qd:32 * qd + 32, 2 * t + k:2 * t + k + 1], T.cnt[64 + 32 * k:96 + 32 * k, 0:1],
-                             T.g2[32 * k:32 * k + 32, 0:1], T.cnt[32 * k:32 * k + 32, 0:1], A.add, A.max,
-                             [v_g2, s_cnt]))
-        v_ro = cp(T.roff[64:128, 2 * t:2 * t + 2], T.roff[0:64, 2 * t:2 * t + 2], rs)
+        for h in range(2):
+            ts(T.roff[64 * h:64 * h + 64, 2 * t:2 * t + 1], T.cnt[64:128, 0:1], T.g2[0:64, 0:1], T.cnt[0:64, 0:1],
+               A.add, A.max, [v_g2, s_cnt])
+        v_ro = None
+        for qd in range(4):
+            k = 1 - qd % 2
+            v_ro = ts(T.roff[32 * qd:32 * qd + 32, 2 * t + 1:2 * t + 2], T.cnt[64 + 32 * k:96 + 32 * k, 0:1],
+                      T.g2[32 * k:32 * k + 32, 0:1], T.cnt[32 * k:32 * k + 32, 0:1], A.add, A.max)
         lo, hi = NL * rank, NL * rank + NL
         v_pk = pickq(laq[:, lo:hi], xq[:, 0:258], T.roff[:, 2 * t:2 * t + 2], [v_ro])
         s_pk = picks(las[:, lo:hi], xs[:, 0:258], T.roff[:, 2 * t:2 * t + 2], [v_ro])
@@ -250,77 +261,80 @@ def rank_program(g, core, T, topo):
         a_s = spread(lambda: las[:, lo:hi], "arrs%d" % t, [s_pk])
 
         if t == 0:
-            b0 = ts(T.fb[0:64, 0:4], T.vi[0:64, 0:4], 0.0, 1.0, A.is_lt, A.add)
-            b1 = ts(T.fb[0:64, 4:5], T.vi[0:64, 5:6], 1.0, 0.0, A.min, A.max)
-            k0 = ts(T.pa7[:, 0:1], T.pint[:, 0:1], 7, None, A.bitwise_and, None, [i_p, i_k])
-            k1 = ts(T.pb1[:, 0:1], T.pint[:, 0:1], 3, 1, A.logical_shift_right, A.bitwise_and)
-            b2 = red(T.scb[0:64, 0:1], T.fb[0:64, 0:5], A.mult, [b0, b1])
-            k2 = ts(T.pf[:, 0:1], T.pa7[:, 0:1], 32.0, None, A.mult, None, [k0])
-            k3 = cp(T.pf[:, 1:2], T.pb1[:, 0:1], [k1])
-            b3 = ts(T.cl[0:32, 0:512:4], T.zz[0:32, 0:128], T.scb[0:32, 0:1], 1.0 / BIT, A.add, A.mult, [b2, s_cl])
-            b4 = ts(T.cl[32:64, 512:1024:4], T.zz[32:64, 0:128], T.scb[32:64, 0:1], 1.0 / BIT, A.add, A.mult)
-            late["coff"] = ts(T.coff[:], T.k2[:], T.pf[:, 0:1], T.pf[:, 1:2], A.add, A.add, [k2, k3])
-            late["lq"] = qz(T.lq[:], T.ls[:], T.cl[:], [b3, b4])
-            e0 = ts(T.vm[:], T.vb[:], 15, None, A.bitwise_and)
+            late["lq"] = qz(T.lq[:], T.ls[:], T.cl[:], lc)
+            k0 = ts(T.pa7[:, 0:1], T.pint[:, 0:1], 3, 225, A.logical_shift_right, A.bitwise_and, [i_k])
+            late["rm8"] = ms(T.rm8[:, 0:256:8], 0.0, [r0])
             for b in range(4):
                 late["eq"] = qz(T.eq[:, 128 * b:128 * b + 128], T.es[:, 128 * b:128 * b + 128],
                                 T.fe[:, 3 - b:515 - b], [t_fe])
-            late["sel"] = ts(T.sel[:], T.vm[:], 0.0, None, A.is_equal, None, [e0])
+            k1 = cp(T.pf[:, 0:1], T.pa7[:, 0:1], [k0])
             act(T.st[:, 1024:1280], T.zz[:], F.Copy)
             act(T.st[:, 1536:1792], T.zz[:], F.Copy)
             repeat(1)
             late["st"] = repeat(2)
-        p_la = mm(bank(T.pb, 3, 128), T.lq, T.ls, 0, T.bq, T.bs, 0, 128, True, True, [late["lq"]])
-        p_lb = mm(bank(T.pb, 0, 128), T.lq, T.ls, 128, T.bq, T.bs, 0, 128, True, True)
+        p_l = [mm(bank(T.pb, h, 128), T.lq, T.ls, 128 * h, T.bq, T.bs, 0, 128, True, True, [late["lq"]])
+               for h in range(2)]
         for b in range(4):
-            mm(bank(T.pa, b, 256), T.eq, T.es, 128 * b, xq, xs, 0, 256, True, False, [late["eq"]])
-        s_la = act(T.lrow[:, 256 * t:256 * t + 128], bank(T.pb, 3, 128), F.Copy, [p_la])
-        s_lb = act(T.lrow[:, 256 * t + 128:256 * t + 256], bank(T.pb, 0, 128), F.Copy, [p_lb])
+            mm(bank(T.pa, b, 128), T.eq, T.es, 128 * b, xq, xs, 2, 128, True, False, [late["eq"], v_pm])
+        l_s = [scan(T.lsc[:, 128 * h:128 * h + 128], T.m16[:], bank(T.pb, h, 128), 0.0, A.min, A.max, [p_l[h], i_m])
+               for h in range(2)]
         if t == 0:
-            for b in range(4):
-                late["fq"] = qz(T.fq[:, 128 * b:128 * b + 128], T.fs[:, 128 * b:128 * b + 128],
-                                T.ff[:, 3 - b:515 - b], [s_ff])
-        l0 = tt(T.lm[:, 0:128], bank(T.pb, 3, 128), T.sel[:], A.mult, [s_la, late["sel"]])
-        l1 = tt(T.lm[:, 128:256], bank(T.pb, 0, 128), T.sel[:], A.mult, [s_lb])
-        l2 = scan(T.lsc[:], T.rm16[:], T.lm[:], 0.0, A.mult, A.add, [l0, l1, t_rm16])
-        off = T.loff[:, 16 * t:16 * t + 16]
-        v_lo = ts(off, T.lsc[:, 15:256:16], 8.0, 7.0, A.mult, A.add, [l2])
+            late["coff"] = ts(T.coff[:], T.k2[:], T.pf[:, 0:1], None, A.add, None, [k1])
+        v_lo = ts(T.loff[:, 16 * t:16 * t + 16], T.lsc[:, 15:256:16], 8.0, 7.0 - 512.0, A.mult, A.add, l_s)
+        s_l = [act(T.lrow[0:1, 256 * t + 128 * h:256 * t + 128 * h + 128], T.pb[0:1, 512 * h:512 * h + 128], F.Copy,
+                   [l_s[h]]) for h in range(2)]
         if t == 0:
             t_sq = qz(T.sq[:, 192:448], T.ss[:, 192:448], T.st[:, 768:1792], [late["st"]])
         if t == 1:
             late["zq"] = qz(T.zq[:], T.zs[:], T.zin[:], [t_z])
         if t == R - 1:
-            dma("Y", T.lv[:], T.lrow[0:1, 0:768], "sto", [s_lb])
+            s_lv = act(T.lrow[0:1, 0:768:16], T.lrow[0:1, 0:768:16], F.Identity, s_l, bias=-64.0)
+            dma("Y", T.lv[:], T.lrow[0:1, 0:768], "sto", [s_lv])
 
-        v_or = pickq(roq[:], laq[:], T.coff[:], [a_c, late["coff"], v_pk])
-        s_or = picks(ros[:], las[:], T.coff[:], [a_s, late["coff"], s_pk])
+        pickq(roq[:, 0:128], laq[:], T.coff[:, 0:8], [a_c, late["coff"], v_pk])
+        pickq(roq[:, 128:256], laq[:], T.coff[:, 8:16])
+        v_or = cp(ros[:, 0:128], las[:].indirect(T.coff[:, 0:8]), [a_s, s_pk])
+        s_or = picks(ros[:, 128:256], las[:], T.coff[:, 8:16], [a_s, late["coff"], s_pk])
         sums = []
         for b in range(4):
             p_d = mm(bank(T.pb, b, 256), T.eq, T.es, 128 * b, roq, ros, 0, 256, True, True, [v_or, s_or])
-            sums.append(scan(T.vt[:, b:1024:4], T.rm8[:], bank(T.pb, b, 256), 0.0, A.mult, A.add, [p_d, t_rm8]))
+            sums.append(scan(T.vt[:, b:1024:4], T.rm8[:], bank(T.pb, b, 256), 0.0, A.mult, A.add, [p_d, late["rm8"]]))
         v_vq = qz(vvq[:], vvs[:], T.vt[:], sums)
-
-        v_vp = pickq(vpq[:], vvq[:], T.loff[:, 16 * t:16 * t + 16], [v_vq, v_lo])
-        s_vp = picks(vps[:], vvs[:], T.loff[:, 16 * t:16 * t + 16], [v_vq, v_lo])
-        outs = []
         for b in range(4):
-            p_s = mm(bank(T.pa, b, 256), T.fq, T.fs, 128 * b, vpq, vps, 0, 256, False, True, [v_vp, s_vp, late["fq"]])
-            if b % 2 == 0:
-                outs.append(act(T.ht[:, b:1024:4], bank(T.pa, b, 256), F.Copy, [p_s], scale=8.0))
+            mm(bank(T.pb, b, 128), T.eq, T.es, 128 * b, xq, xs, 130, 128, True, False, [sums[b]])
+
+        picked = []
+        for h in range(2):
+            off = T.loff[:, 16 * t + 8 * h:16 * t + 8 * h + 8]
+            picked.append([pickq(vpq[:, 128 * h:128 * h + 128], vvq[:], off, [v_vq, v_lo]),
+                           picks(vps[:, 128 * h:128 * h + 128], vvs[:], off, [v_vq, v_lo])])
+        new = []
+        for h in range(2):
+            ps = (T.pa, T.pb)[h]
+            outs = []
+            for b in range(4):
+                p_s = mm(bank(ps, b, 128), T.eq, T.es, 128 * b, vpq, vps, 128 * h, 128, False, True, picked[h])
+                dst = T.ht[:, 8 + 512 * h + b:520 + 512 * h:4]
+                if (h, b) in ((0, 0), (0, 2), (1, 3)):
+                    outs.append(ts(dst, bank(ps, b, 128), 1 / UNP, None, A.mult, None, [p_s]))
+                else:
+                    outs.append(act(dst, bank(ps, b, 128), F.Copy, [p_s], scale=1 / UNP))
+            if h == 0:
+                new.append(qz(nq[:, 0:130], ns[:, 0:130], T.ht[:, 0:520], outs + [t_ht]))
             else:
-                outs.append(ts(T.ht[:, b:1024:4], bank(T.pa, b, 256), 8.0, None, A.mult, None, [p_s]))
-        x_a = qz(nq[:, 0:128], ns[:, 0:128], T.ht[:, 0:512], outs)
-        x_b = qz(nq[:, 128:258], ns[:, 128:258], T.ht[:, 512:1032], [t_ht])
+                new.append(qz(nq[:, 130:258], ns[:, 130:258], T.ht[:, 520:1032], outs))
+        x_a, x_b = new
 
     xq, xs = T["xq%d" % R], T["xs%d" % R]
-    p_ya = mm(bank(T.pb, 0, 128), T.zq, T.zs, 0, xq, xs, 0, 128, True, True, [x_a, late["zq"]])
-    p_yb = mm(bank(T.pb, 1, 128), T.zq, T.zs, 0, xq, xs, 128, 128, True, True, [x_b])
-    dma("Y", T.oc[:, 0:4 * TC], xq[:, 0:TC].bitcast(dt.uint8), "sto", [x_b])
+    p_ya = mm(bank(T.pa, 0, 128), T.zq, T.zs, 0, xq, xs, 2, 128, True, True, [x_a, late["zq"]])
+    p_yb = mm(bank(T.pa, 1, 128), T.zq, T.zs, 0, xq, xs, 130, 128, True, True, [x_b])
+    dma("Y", T.oc[:, 0:512], xq[:, 2:130].bitcast(dt.uint8), "sto", [x_a])
+    s_ya = act(T.yo[:, 0:128], bank(T.pa, 0, 128), F.Copy, [p_ya])
+    dma("S", T.y[:, 0:128], T.yo[:, 0:128], "sto", [s_ya])
+    dma("Y", T.oc[:, 512:1024], xq[:, 130:258].bitcast(dt.uint8), "sto", [x_b])
     for k in range(4):
-        dma("Y" if k < 2 else "S", T.osc[4 * k:4 * k + 4, 0:TC], xs[32 * k:32 * k + 4, 0:TC], "sto", [x_b])
-    v_ya = cp(T.yo[:, 0:128], bank(T.pb, 0, 128), [p_ya])
-    v_yb = cp(T.yo[:, 128:256], bank(T.pb, 1, 128), [p_yb])
-    dma("Y", T.y[:, 0:128], T.yo[:, 0:128], "sto", [v_ya])
-    dma("S", T.y[:, 128:256], T.yo[:, 128:256], "sto", [v_yb])
+        dma("Y" if k < 2 else "S", T.osc[4 * k:4 * k + 4, 0:TC], xs[32 * k:32 * k + 4, 2:2 + TC], "sto", [x_b])
+    v_yb = cp(T.yo[:, 128:256], bank(T.pa, 1, 128), [p_yb])
+    dma("Y", T.y[:, 128:256], T.yo[:, 128:256], "sto", [v_yb])
     wait("G", *[(s, count[s]) for s in ("sent", "sg", "sp", "sa", "sv")])
     wait("Y", ("sto", count["sto"]))

@@ -4,34 +4,39 @@ from concourse.mybir import dt, AluOpType, AxisListType, ActivationFunctionType
 R = 3
 TC = 256
 NL = 32
+Z0 = 128
+X0 = Z0 + 2
 Q8 = "float8_e4m3fn_x4"
+ORDER_V = (0, 2, 4, 1, 6, 3, 7, 5)
+VIA = (1, 3, 5)
+STEP_V = (((0, 0), (0, 2), (1, 0), (1, 2)), ((0, 0), (0, 2), (1, 3)))
 
 
 def _scratch():
     s = {}
     for name, cols in (("xin", 1032),
                        ("ht", 1032),
-                       ("ut", 704),
-                       ("st", 1792),
+                       ("ut", 576),
+                       ("st", 1536),
                        ("zin", 512), ("zz", 256),
                        ("ct", 512),
-                       ("cl", 1024),
+                       ("cl", 512),
                        ("fe", 520),
-                       ("rm8", 256), ("vb", 128),
-                       ("bt", 512),
+                       ("rm8", 128), ("vb", 128), ("cv", 1024),
+                       ("bt", 1024),
                        ("vt", 1024)):
         s[name] = ("sbuf", [128, cols], "bfloat16")
-    for name, cols in (("vi", 8), ("li", 64), ("fa", 8), ("fb", 8), ("sca", 4), ("scb", 4), ("m16", 128),
-                       ("pf", 4), ("k2", 16), ("pm", 132), ("junk", 132),
+    for name, cols in (("vi", 8), ("li", 128), ("fa", 8), ("fb", 8), ("sca", 4), ("scb", 4), ("m16", 128),
+                       ("pf", 4), ("k2", 16), ("pm", 264), ("junk", 264),
                        ("cnt", 4), ("g1", 4), ("g2", 4), ("lrow", 768), ("lsc", 256), ("yo", 256)):
         s[name] = ("sbuf", [128, cols], "float32")
-    for name, cols in (("yi", 64), ("yb", 64), ("pint", 4), ("pa7", 4)):
+    for name, cols in (("yi", 128), ("yb", 128), ("pint", 4), ("pa7", 4)):
         s[name] = ("sbuf", [128, cols], "int32")
     for name, cols in (("coff", 16), ("roff", 8), ("loff", 48)):
         s[name] = ("sbuf", [128, cols], "uint16")
-    pairs = [("uq", "us", 176), ("sq", "ss", 448), ("zq", "zs", 128), ("cq", "cs", 128), ("lq", "ls", 256),
-             ("eq", "es", 512), ("bq", "bs", 128)]
-    pairs += [("xq%d" % t, "xs%d" % t, 258) for t in range(R + 1)]
+    pairs = [("uq", "us", 144), ("sq", "ss", 384), ("zq", "zs", 128), ("cq", "cs", 128), ("lq", "ls", 128),
+             ("eq", "es", 512), ("bq", "bs", 256)]
+    pairs += [("xq%d" % t, "xs%d" % t, X0 + TC) for t in range(R + 1)]
     pairs += [("%sq%d" % (n, t), "%ss%d" % (n, t), 256) for t in range(R) for n in ("la", "ro", "vv", "vp")]
     for q, p, cols in pairs:
         s[q] = ("sbuf", [128, cols], Q8)
@@ -103,9 +108,9 @@ def rank_program(g, core, T, topo):
         wait("S", *deps)
         return done(g.scalar.activation(out, in_, func, **kw), "sa")
 
-    def mm(out, lq, ls, a, rq, rs, b, w, start, stop, deps=()):
+    def mm(out, lq, ls, a, rq, rs, b, start, stop, deps=()):
         wait("P", *deps)
-        return done(g.tensor.matmul_mx(out, lq[:, a:a + 128], ls[:, a:a + 128], rq[:, b:b + w], rs[:, b:b + w],
+        return done(g.tensor.matmul_mx(out, lq[:, a:a + 128], ls[:, a:a + 128], rq[:, b:b + 128], rs[:, b:b + 128],
                                        start, stop), "sp")
 
     def iota(out, pattern, base, cm, small, deps=()):
@@ -124,23 +129,24 @@ def rank_program(g, core, T, topo):
     def picks(out, win, off, deps=()):
         return act(out, win.indirect(off), F.Copy, deps)
 
-    def bank(buf, b, w):
-        return buf[:, 512 * b:512 * b + w]
+    def bank(buf, b):
+        return buf[:, 512 * b:512 * b + 128]
+
+    def state(t, h, tile, deps):
+        a, b = (Z0, X0 + 128) if h == 0 else (X0 + 128, X0 + TC)
+        return qz(T["xq%d" % t][:, a:b], T["xs%d" % t][:, a:b], tile[:, 4 * (a - Z0):4 * (b - Z0)], deps)
 
     others = [cores[(rank + k) % n] for k in range(1, n)]
-    mask = topo.mask(core, others[0])
-    for o in others[1:]:
-        mask = mask & topo.mask(core, o)
-    lanes = bin(mask).count("1")
+    lanes = [e for e in topo.engines(core, others[0]) if all(e in topo.engines(core, o) for o in others)]
     ids = [DstId(rid=topo.addr(o)[0], pnc=topo.addr(o)[1]) for o in others]
 
     def spread(view, sem, deps):
         wait("G", *deps)
-        tr = RemoteDMATransfer(dst_ids=ids, dma_engine_mask=mask, remote_sem=T.sem[sem],
+        tr = RemoteDMATransfer(dst_ids=ids, dma_engine_mask=sum(1 << e for e in lanes), remote_sem=T.sem[sem],
                                srcs=[view()], dsts=[view() for o in others])
         g.remote_dma_fused([tr], local_sem=T.sem.sent)
-        count["sent"] = count.get("sent", 0) + lanes
-        return (sem, lanes * (n - 1))
+        count["sent"] = count.get("sent", 0) + len(lanes)
+        return (sem, len(lanes) * (n - 1))
 
     BIT = 2.0 ** 30
     PEN = 2.0 ** 42
@@ -148,69 +154,65 @@ def rank_program(g, core, T, topo):
     UNP = -0.0625
 
     t_xa = dma("S", T.xin[:, 8:520], T.x[:, 0:512], "lxa")
-    t_w = dma("Y", T.ut[:, 128:224], T.w[:, 0:96], "lw")
+    t_w = dma("Y", T.ut[:, 0:96], T.w[:, 0:96], "lw")
     t_xb = dma("Y", T.xin[:, 520:1032], T.x[:, 512:1024], "lxb")
     t_z = dma("Y", T.zin[:], T.z[:], "lz", [t_xb])
 
-    i_v0 = iota(T.vi[32:64, 0:4], [[1, 4]], 2, -1, True)
     i_v = iota(T.vi[0:32, 0:4], [[1, 4]], 2, -1, True)
-    i_l = iota(T.li[0:64, :], [[16, 2], [0, 2], [1, 16]], 0, 0, True, [i_v0])
+    i_l = iota(T.li[0:32, :], [[16, 2], [0, 4], [1, 16]], 0, 0, True)
 
     t_zz = ms(T.zz[:], 0.0)
-    t_b1 = ms(T.bt[:, 1:512:4], BIT)
-    ms(T.bt[96:128, 0:512:4], 0.0)
-    ms(T.ut[:, 0:128], 0.0)
-    t_ut = ms(T.ut[:, 224:704], 0.0)
-    t_ct = ms(T.ct[:], 0.0)
-    wait("G", t_b1, i_l)
-    i_sel = done(g.affine_select(T.bt[64:96, 0:512:4], T.bt[64:96, 1:512:4], [[0, 8], [1, 16]], A.is_equal, 0.0, 0, -1),
-                 "sg")
+    ms(T.bt[:, 0:1024:4], 0.0)
+    t_b1 = ms(T.bt[:, 1:1024:4], BIT)
+    wait("G", t_b1)
+    i_sel = done(g.affine_select(T.bt[64:96, 0:1024:4], T.bt[64:96, 1:1024:4], [[0, 16], [1, 16]], A.is_equal, 0.0,
+                                 0, -1), "sg")
     i_vb = iota(T.vb[:], [[1, 128]], 0, -1, True, [i_sel])
     iota(T.pint[:, 0:1], [[0, 1]], 0, 257, False)
     i_m = iota(T.m16[:], [[0, 8], [100, 16]], 0, 0, True)
     i_k = iota(T.k2[:], [[2, 16]], 0, 0, True)
-    for qd in (1, 3):
-        i_k = iota(T.k2[32 * qd:32 * qd + 32, :], [[-16, 2], [2, 8]], 16, 0, True, [i_k])
+    i_k = iota(T.k2[64:128, :], [[-16, 2], [2, 8]], 16, 0, True, [i_k])
 
-    s_z0 = act(T.st[:, 0:256], T.zz[:], F.Copy, [t_zz])
-    s_z1 = act(T.st[:, 512:768], T.zz[:], F.Copy)
-    act(T.bt[:, 2:512:4], T.zz[:, 0:128], F.Copy)
-    s_bt = act(T.bt[:, 3:512:4], T.zz[:, 0:128], F.Copy)
-    a0 = ts(T.fa[0:64, 0:4], T.vi[0:64, 0:4], 2.0, 1.0, A.min, A.max, [i_v])
-    a1 = ts(T.fa[0:64, 4:5], T.vi[0:64, 3:4], 1.0, PEN / 8, A.is_ge, A.mult)
+    act(T.ut[:, 96:336], T.zz[:, 0:240], F.Copy, [t_zz])
+    s_ut = act(T.ut[:, 336:576], T.zz[:, 0:240], F.Copy)
+    act(T.bt[:, 2:1024:4], T.zz[:], F.Copy)
+    s_bt = act(T.bt[:, 3:1024:4], T.zz[:], F.Copy)
+    act(T.cl[:, 0:256], T.zz[:], F.Copy)
+    s_cl = act(T.cl[:, 256:512], T.zz[:], F.Copy)
+    a0 = ts(T.fa[0:32, 0:4], T.vi[0:32, 0:4], 2.0, 1.0, A.min, A.max, [i_v])
+    a1 = ts(T.fa[0:32, 4:5], T.vi[0:32, 3:4], 1.0, PEN / 8, A.is_ge, A.mult)
     t_xt = ms(T.xin[:, 0:8], 0.0)
-    a2 = red(T.sca[0:64, 0:1], T.fa[0:64, 0:5], A.mult, [a0, a1])
-    t_pm = ms(T.pm[:, 0:2], LOW)
-    a3 = ts(T.yi[0:64, :], T.li[0:64, :], T.sca[0:64, 0:1], 8 / PEN, A.mult, A.mult, [a2, i_l])
+    ms(T.pm[:, 0:2], LOW)
+    a2 = red(T.sca[0:32, 0:1], T.fa[0:32, 0:5], A.mult, [a0, a1])
+    t_pm = ms(T.pm[:, 132:134], LOW)
     t_ht = ms(T.ht[:, 0:8], 0.0)
-    a4 = ts(T.yb[0:64, :], T.yi[0:64, :], 16, None, A.bitwise_and, None, [a3])
-    b0 = ts(T.fb[0:64, 0:4], T.vi[0:64, 0:4], 2.0, 1.0, A.is_lt, A.add)
-    cs = []
-    for h in range(2):
-        lo = 32 * h
-        cs.append(ts(T.ct[lo:lo + 32, 256 * h:256 * h + 256:4], T.yb[lo:lo + 32, :], -8.0, T.fa[lo:lo + 32, 4:5],
-                     A.add, A.mult, [a4, t_ct]))
-        cs.append(ts(T.ct[lo:lo + 32, 256 * h + 1:256 * h + 256:4], T.yb[lo:lo + 32, :], -PEN / 16, None, A.mult))
-    b1 = ts(T.fb[0:64, 4:5], T.vi[0:64, 3:4], 1.0, 1.0 / (BIT * BIT), A.is_ge, A.mult)
-    t_cq = qz(T.cq[:], T.cs[:], T.ct[:], cs)
-    b2 = red(T.scb[0:64, 0:1], T.fb[0:64, 0:5], A.mult, [b0, b1])
+    a3 = ts(T.yi[0:32, :], T.li[0:32, :], T.sca[0:32, 0:1], 8 / PEN, A.mult, A.mult, [a2, i_l])
+    t_ct = ms(T.ct[:], 0.0)
+    a4 = ts(T.yb[0:32, :], T.yi[0:32, :], 16, None, A.bitwise_and, None, [a3])
+    b0 = ts(T.fb[0:32, 0:4], T.vi[0:32, 0:4], 2.0, 1.0, A.is_lt, A.add)
+    b1 = ts(T.fb[0:32, 4:5], T.vi[0:32, 3:4], 1.0, 1.0 / (BIT * BIT), A.is_ge, A.mult)
+    r0 = ms(T.rm8[:], 1.0)
+    c0 = ts(T.ct[0:32, 0:512:4], T.yb[0:32, :], -8.0, T.fa[0:32, 4:5], A.add, A.mult, [a4, t_ct])
+    c1 = ts(T.ct[0:32, 1:512:4], T.yb[0:32, :], -PEN / 16, None, A.mult)
+    b2 = red(T.scb[0:32, 0:1], T.fb[0:32, 0:5], A.mult, [b0, b1])
+    t_rm8 = ms(T.rm8[:, 0:128:8], 0.0, [r0])
+    t_cq = qz(T.cq[:], T.cs[:], T.ct[:], [c0, c1])
 
     def repeat(t):
         tok = None
         for e in range(4):
-            lo = 4 * (64 + 128 * t)
-            col = 128 + 4 * (8 * t + 6) + e
-            tok = act(T.st[:, lo + e:lo + 256:4], T.zz[:, 0:64], F.Identity, [t_w], bias=T.ut[:, col:col + 1])
+            col = 4 * (8 * t + 6) + e
+            tok = act(T.st[:, 512 * t + e:512 * t + 512:4], T.zz[:, 0:128], F.Identity, [t_w],
+                      bias=T.ut[:, col:col + 1])
         return tok
 
     s_r0 = repeat(0)
-    s_cl = None
-    for k in range(4):
-        s_cl = act(T.cl[:, 256 * k:256 * k + 256], T.zz[:], F.Copy)
-    t_uq = qz(T.uq[:], T.us[:], T.ut[:], [t_w, t_ut])
-    x_a = qz(T.xq0[:, 0:130], T.xs0[:, 0:130], T.xin[:, 0:520], [t_xa, t_xt])
-    t_sq = qz(T.sq[:, 0:192], T.ss[:, 0:192], T.st[:, 0:768], [s_r0, s_z0, s_z1])
-    x_b = qz(T.xq0[:, 130:258], T.xs0[:, 130:258], T.xin[:, 520:1032], [t_xb])
+    lc = [act(T.cl[0:32, 0:512:4], T.bt[0:32, 1:512:4], F.Identity, [s_cl, b2], scale=T.scb[0:32, 0:1]),
+          act(T.cl[64:96, 0:512:4], T.bt[64:96, 0:512:4], F.Copy, [i_sel], scale=64.0 / (BIT * BIT))]
+    t_uq = qz(T.uq[:], T.us[:], T.ut[:], [t_w, s_ut])
+    x_a = state(0, 0, T.xin, [t_xa, t_xt])
+    x_b = state(0, 1, T.xin, [t_xb])
+    t_sq = qz(T.sq[:, 0:128], T.ss[:, 0:128], T.st[:, 0:512], [s_r0])
 
     late = {}
     for t in range(R):
@@ -219,122 +221,123 @@ def rank_program(g, core, T, topo):
         roq, ros = T["roq%d" % t], T["ros%d" % t]
         vvq, vvs = T["vvq%d" % t], T["vvs%d" % t]
         vpq, vps = T["vpq%d" % t], T["vps%d" % t]
-        nq, ns = T["xq%d" % (t + 1)], T["xs%d" % (t + 1)]
+        pe, pl = (T.pa, T.pb) if t % 2 == 0 else (T.pb, T.pa)
 
-        mm(bank(T.pa, 0, 128), T.uq, T.us, 32 + 8 * t, xq, xs, 2, 128, True, False, [t_uq, x_a])
-        mm(bank(T.pa, 1, 128), T.sq, T.ss, 64 + 128 * t, xq, xs, 2, 128, True, False, [t_sq])
-        p_pl = mm(bank(T.pa, 0, 128), T.uq, T.us, 8 * t, xq, xs, 130, 128, False, True, [x_b])
-        mm(bank(T.pa, 1, 128), T.sq, T.ss, 128 * t, xq, xs, 130, 128, False, False)
+        p_pl = [mm(bank(pe, h), T.uq, T.us, 8 * t, xq, xs, X0 + 128 * h, True, True, [t_uq, (x_a, x_b)[h]])
+                for h in range(2)]
+        for h in range(2):
+            mm(bank(pe, 2 + h), T.sq, T.ss, 128 * t, xq, xs, X0 + 128 * h, True, False, [t_sq])
+        v_lt = [ts(T.bt[0:32, 512 * h:512 * h + 512:4], pe[0:32, 512 * h:512 * h + 128], 0.0, BIT, A.is_lt, A.mult,
+                   [p_pl[h]]) for h in range(2)]
+        v_bq = [qz(T.bq[:, 128 * h:128 * h + 128], T.bs[:, 128 * h:128 * h + 128], T.bt[:, 512 * h:512 * h + 512],
+                   [v_lt[h], s_bt, i_sel]) for h in range(2)]
+        p_pen = [mm(bank(pe, 2 + h), T.cq, T.cs, 0, T.bq, T.bs, 128 * h, False, True, [v_bq[h], t_cq])
+                 for h in range(2)]
         if t == 0:
             t_fe0 = ms(T.fe[:], 0.0)
-        v_lt = ts(T.bt[0:64, 0:512:4], T.pa[0:64, 0:128], 0.0, BIT, A.is_lt, A.mult, [p_pl])
-        v_bq = qz(T.bq[:], T.bs[:], T.bt[:], [v_lt, s_bt, i_sel])
-        p_pen = mm(bank(T.pa, 1, 128), T.cq, T.cs, 0, T.bq, T.bs, 0, 128, False, True, [v_bq, t_cq])
+        v_pm, s_cnt = [], []
+        for h in range(2):
+            at = 132 * h
+            v_pm.append(scan(T.pm[:, at + 2:at + 130], bank(pe, 2 + h), T.zz[:, 0:128], LOW, A.max, A.add,
+                             [p_pen[h], t_pm]))
+            s_cnt.append(act(T.junk[:, at:at + 130], T.pm[:, at:at + 130], F.Sign, [v_pm[h]],
+                             bias=T.pm[:, at + 129:at + 130], scale=-1.0, accum_out=T.cnt[:, h:h + 1]))
         if t == 0:
             t_fe = ts(T.fe[:, 3:515:4], T.vb[:], 0.0, UNP, A.is_equal, A.mult, [t_fe0, i_vb])
-            r0 = ms(T.rm8[:], 1.0)
-            lc = []
-            for h in range(2):
-                lo = 32 * h
-                lc.append(act(T.cl[lo:lo + 32, 512 * h:512 * h + 512:4], T.bt[lo:lo + 32, 1:512:4], F.Identity,
-                              [s_cl, b2], scale=T.scb[lo:lo + 32, 0:1]))
-                lc.append(act(T.cl[64:96, 512 * h:512 * h + 512:4], T.bt[64:96, 0:512:4], F.Copy, [i_sel],
-                              scale=64.0 / (BIT * BIT)))
-        v_pm = scan(T.pm[:, 2:130], bank(T.pa, 1, 128), T.zz[:, 0:128], LOW, A.max, A.add, [p_pen, t_pm])
-        s_cnt = act(T.junk[:, 0:130], T.pm[:, 0:130], F.Sign, [v_pm], bias=T.pm[:, 129:130], scale=-1.0,
-                    accum_out=T.cnt[:, 0:1])
-        v_g1 = ts(T.g1[0:64, 0:1], T.pm[64:128, 129:130], T.pm[0:64, 129:130], 512.0, A.is_gt, A.mult, [v_pm])
-        v_g2 = ts(T.g2[0:64, 0:1], T.g1[0:64, 0:1], -384.0, None, A.add, None, [v_g1])
-        for h in range(2):
-            ts(T.roff[64 * h:64 * h + 64, 2 * t:2 * t + 1], T.cnt[64:128, 0:1], T.g2[0:64, 0:1], T.cnt[0:64, 0:1],
-               A.add, A.max, [v_g2, s_cnt])
+        v_g1 = ts(T.g1[:, 0:1], T.pm[:, 261:262], T.pm[:, 129:130], Z0 + 128.0, A.is_gt, A.mult, v_pm)
+        v_g2 = ts(T.g2[:, 0:1], T.cnt[:, 0:1], float(Z0), None, A.add, None, [s_cnt[0]])
         v_ro = None
-        for qd in range(4):
-            k = 1 - qd % 2
-            v_ro = ts(T.roff[32 * qd:32 * qd + 32, 2 * t + 1:2 * t + 2], T.cnt[64 + 32 * k:96 + 32 * k, 0:1],
-                      T.g2[32 * k:32 * k + 32, 0:1], T.cnt[32 * k:32 * k + 32, 0:1], A.add, A.max)
+        for col, a, b, w in ((0, 0, 0, 128), (1, 0, 64, 64), (1, 64, 0, 64)):
+            v_ro = ts(T.roff[a:a + w, 2 * t + col:2 * t + col + 1], T.cnt[b:b + w, 1:2], T.g1[b:b + w, 0:1],
+                      T.g2[b:b + w, 0:1], A.add, A.max, [v_g1, v_g2, s_cnt[1]])
         lo, hi = NL * rank, NL * rank + NL
-        v_pk = pickq(laq[:, lo:hi], xq[:, 0:258], T.roff[:, 2 * t:2 * t + 2], [v_ro])
-        s_pk = picks(las[:, lo:hi], xs[:, 0:258], T.roff[:, 2 * t:2 * t + 2], [v_ro])
+        v_pk = pickq(laq[:, lo:hi], xq[:], T.roff[:, 2 * t:2 * t + 2], [v_ro])
+        s_pk = picks(las[:, lo:hi], xs[:], T.roff[:, 2 * t:2 * t + 2], [v_ro])
 
         a_c = spread(lambda: laq[:, lo:hi].bitcast(dt.uint8), "arrc%d" % t, [v_pk])
         a_s = spread(lambda: las[:, lo:hi], "arrs%d" % t, [s_pk])
 
         if t == 0:
-            late["lq"] = qz(T.lq[:], T.ls[:], T.cl[:], lc)
             k0 = ts(T.pa7[:, 0:1], T.pint[:, 0:1], 3, 225, A.logical_shift_right, A.bitwise_and, [i_k])
-            late["rm8"] = ms(T.rm8[:, 0:256:8], 0.0, [r0])
+            late["lq"] = qz(T.lq[:], T.ls[:], T.cl[:], lc)
+            k1 = cp(T.pf[:, 0:1], T.pa7[:, 0:1], [k0])
             for b in range(4):
                 late["eq"] = qz(T.eq[:, 128 * b:128 * b + 128], T.es[:, 128 * b:128 * b + 128],
                                 T.fe[:, 3 - b:515 - b], [t_fe])
-            k1 = cp(T.pf[:, 0:1], T.pa7[:, 0:1], [k0])
-            act(T.st[:, 1024:1280], T.zz[:], F.Copy)
-            act(T.st[:, 1536:1792], T.zz[:], F.Copy)
+            late["coff"] = ts(T.coff[:], T.k2[:], T.pf[:, 0:1], None, A.add, None, [k1])
             repeat(1)
             late["st"] = repeat(2)
-        p_l = [mm(bank(T.pb, h, 128), T.lq, T.ls, 128 * h, T.bq, T.bs, 0, 128, True, True, [late["lq"]])
+        p_l = [mm(bank(pl, h), T.lq, T.ls, 0, T.bq, T.bs, 128 * h, True, True, [late["lq"]]) for h in range(2)]
+        l_s = [scan(T.lsc[:, 128 * h:128 * h + 128], T.m16[:], bank(pl, h), 0.0, A.min, A.max, [p_l[h], i_m])
                for h in range(2)]
-        for b in range(4):
-            mm(bank(T.pa, b, 128), T.eq, T.es, 128 * b, xq, xs, 2, 128, True, False, [late["eq"], v_pm])
-        l_s = [scan(T.lsc[:, 128 * h:128 * h + 128], T.m16[:], bank(T.pb, h, 128), 0.0, A.min, A.max, [p_l[h], i_m])
-               for h in range(2)]
+        s_l = [act(T.lrow[0:1, 256 * t + 128 * h:256 * t + 128 * h + 128],
+                   pl[0:1, 512 * h:512 * h + 128], F.Copy, [l_s[h]]) for h in range(2)]
         if t == 0:
-            late["coff"] = ts(T.coff[:], T.k2[:], T.pf[:, 0:1], None, A.add, None, [k1])
-        v_lo = ts(T.loff[:, 16 * t:16 * t + 16], T.lsc[:, 15:256:16], 8.0, 7.0 - 512.0, A.mult, A.add, l_s)
-        s_l = [act(T.lrow[0:1, 256 * t + 128 * h:256 * t + 128 * h + 128], T.pb[0:1, 512 * h:512 * h + 128], F.Copy,
-                   [l_s[h]]) for h in range(2)]
-        if t == 0:
-            t_sq = qz(T.sq[:, 192:448], T.ss[:, 192:448], T.st[:, 768:1792], [late["st"]])
+            t_sq = qz(T.sq[:, 128:384], T.ss[:, 128:384], T.st[:, 512:1536], [late["st"]])
         if t == 1:
             late["zq"] = qz(T.zq[:], T.zs[:], T.zin[:], [t_z])
+        v_lo = ts(T.loff[:, 16 * t:16 * t + 16], T.lsc[:, 15:256:16], 8.0, 7.0 - 512.0, A.mult, A.add, l_s)
         if t == R - 1:
             s_lv = act(T.lrow[0:1, 0:768:16], T.lrow[0:1, 0:768:16], F.Identity, s_l, bias=-64.0)
             dma("Y", T.lv[:], T.lrow[0:1, 0:768], "sto", [s_lv])
 
         pickq(roq[:, 0:128], laq[:], T.coff[:, 0:8], [a_c, late["coff"], v_pk])
         pickq(roq[:, 128:256], laq[:], T.coff[:, 8:16])
-        v_or = cp(ros[:, 0:128], las[:].indirect(T.coff[:, 0:8]), [a_s, s_pk])
-        s_or = picks(ros[:, 128:256], las[:], T.coff[:, 8:16], [a_s, late["coff"], s_pk])
-        sums = []
-        for b in range(4):
-            p_d = mm(bank(T.pb, b, 256), T.eq, T.es, 128 * b, roq, ros, 0, 256, True, True, [v_or, s_or])
-            sums.append(scan(T.vt[:, b:1024:4], T.rm8[:], bank(T.pb, b, 256), 0.0, A.mult, A.add, [p_d, late["rm8"]]))
-        v_vq = qz(vvq[:], vvs[:], T.vt[:], sums)
-        for b in range(4):
-            mm(bank(T.pb, b, 128), T.eq, T.es, 128 * b, xq, xs, 130, 128, True, False, [sums[b]])
+        put = [[cp(ros[:, 0:128], las[:].indirect(T.coff[:, 0:8]), [a_s, s_pk])] + s_l,
+               [picks(ros[:, 128:256], las[:], T.coff[:, 8:16], [a_s, late["coff"], s_pk])]]
+        p_d, freed, sums = {}, {}, {}
+        for k in range(8):
+            h, b = divmod(k, 4)
+            p_d[k] = mm(bank((pl, pe)[h], b), T.eq, T.es, 128 * b, roq, ros, 128 * h, True, True,
+                        put[h] + [late["eq"]])
+            if k in VIA:
+                freed[k] = act(T.cv[:, 128 * k:128 * k + 128], bank((pl, pe)[h], b), F.Copy, [p_d[k]])
+        for k in ORDER_V:
+            h, b = divmod(k, 4)
+            dst = T.vt[:, 512 * h + b:512 * h + 512:4]
+            if k in VIA:
+                sums[k] = scan(dst, T.rm8[:], T.cv[:, 128 * k:128 * k + 128], 0.0, A.mult, A.add, [freed[k]])
+            else:
+                sums[k] = freed[k] = scan(dst, T.rm8[:], bank((pl, pe)[h], b), 0.0, A.mult, A.add, [p_d[k], t_rm8])
+        v_vq = None
+        for h in range(2):
+            v_vq = qz(vvq[:, 128 * h:128 * h + 128], vvs[:, 128 * h:128 * h + 128], T.vt[:, 512 * h:512 * h + 512],
+                      [sums[4 * h + b] for b in range(4)])
+        for k in range(8):
+            h, b = divmod(k, 4)
+            mm(bank((pl, pe)[h], b), T.eq, T.es, 128 * b, xq, xs, X0 + 128 * h, True, False, [freed[k]])
 
         picked = []
         for h in range(2):
             off = T.loff[:, 16 * t + 8 * h:16 * t + 8 * h + 8]
             picked.append([pickq(vpq[:, 128 * h:128 * h + 128], vvq[:], off, [v_vq, v_lo]),
                            picks(vps[:, 128 * h:128 * h + 128], vvs[:], off, [v_vq, v_lo])])
-        new = []
+        last = t == R - 1
+        outs = [[t_ht], []]
         for h in range(2):
-            ps = (T.pa, T.pb)[h]
-            outs = []
+            ps = (pl, pe)[h]
             for b in range(4):
-                p_s = mm(bank(ps, b, 128), T.eq, T.es, 128 * b, vpq, vps, 128 * h, 128, False, True, picked[h])
+                p_s = mm(bank(ps, b), T.eq, T.es, 128 * b, vpq, vps, 128 * h, False, True, picked[h])
                 dst = T.ht[:, 8 + 512 * h + b:520 + 512 * h:4]
-                if (h, b) in ((0, 0), (0, 2), (1, 3)):
-                    outs.append(ts(dst, bank(ps, b, 128), 1 / UNP, None, A.mult, None, [p_s]))
+                if (h, b) in STEP_V[last]:
+                    outs[h].append(ts(dst, bank(ps, b), 1 / UNP, None, A.mult, None, [p_s]))
                 else:
-                    outs.append(act(dst, bank(ps, b, 128), F.Copy, [p_s], scale=1 / UNP))
-            if h == 0:
-                new.append(qz(nq[:, 0:130], ns[:, 0:130], T.ht[:, 0:520], outs + [t_ht]))
-            else:
-                new.append(qz(nq[:, 130:258], ns[:, 130:258], T.ht[:, 520:1032], outs))
-        x_a, x_b = new
+                    outs[h].append(act(dst, bank(ps, b), F.Copy, [p_s], scale=1 / UNP))
+            if h == 1 - last:
+                x_a = state(t + 1, 0, T.ht, outs[0])
+        x_b = state(t + 1, 1, T.ht, outs[1])
 
     xq, xs = T["xq%d" % R], T["xs%d" % R]
-    p_ya = mm(bank(T.pa, 0, 128), T.zq, T.zs, 0, xq, xs, 2, 128, True, True, [x_a, late["zq"]])
-    p_yb = mm(bank(T.pa, 1, 128), T.zq, T.zs, 0, xq, xs, 130, 128, True, True, [x_b])
-    dma("Y", T.oc[:, 0:512], xq[:, 2:130].bitcast(dt.uint8), "sto", [x_a])
-    s_ya = act(T.yo[:, 0:128], bank(T.pa, 0, 128), F.Copy, [p_ya])
+    pe = T.pa if R % 2 == 0 else T.pb
+    p_ya = mm(bank(pe, 0), T.zq, T.zs, 0, xq, xs, X0, True, True, [x_a, late["zq"]])
+    p_yb = mm(bank(pe, 1), T.zq, T.zs, 0, xq, xs, X0 + 128, True, True, [x_b])
+    dma("Y", T.oc[:, 0:512], xq[:, X0:X0 + 128].bitcast(dt.uint8), "sto", [x_a])
+    s_ya = act(T.yo[:, 0:128], bank(pe, 0), F.Copy, [p_ya])
     dma("S", T.y[:, 0:128], T.yo[:, 0:128], "sto", [s_ya])
-    dma("Y", T.oc[:, 512:1024], xq[:, 130:258].bitcast(dt.uint8), "sto", [x_b])
+    dma("Y", T.oc[:, 512:1024], xq[:, X0 + 128:X0 + TC].bitcast(dt.uint8), "sto", [x_b])
     for k in range(4):
-        dma("Y" if k < 2 else "S", T.osc[4 * k:4 * k + 4, 0:TC], xs[32 * k:32 * k + 4, 2:2 + TC], "sto", [x_b])
-    v_yb = cp(T.yo[:, 128:256], bank(T.pa, 1, 128), [p_yb])
+        dma("Y" if k < 2 else "S", T.osc[4 * k:4 * k + 4, 0:TC], xs[32 * k:32 * k + 4, X0:X0 + TC], "sto", [x_b])
+    v_yb = cp(T.yo[:, 128:256], bank(pe, 1), [p_yb])
     dma("Y", T.y[:, 128:256], T.yo[:, 128:256], "sto", [v_yb])
     wait("G", *[(s, count[s]) for s in ("sent", "sg", "sp", "sa", "sv")])
     wait("Y", ("sto", count["sto"]))

from concourse.bass import DstId, RemoteDMATransfer
from concourse.mybir import dt, AluOpType, AxisListType, ActivationFunctionType

R = 3
TC = 256
NL = 32
Z0 = 128
X0 = Z0 + 2
Q8 = "float8_e4m3fn_x4"
ORDER_V = (0, 2, 4, 1, 6, 3, 7, 5)
VIA = (1, 3, 5)
STEP_V = (((0, 0), (0, 2), (1, 0), (1, 2)), ((0, 0), (0, 2), (1, 3)))


def _scratch():
    s = {}
    for name, cols in (("xin", 1032),
                       ("ht", 1032),
                       ("ut", 576),
                       ("st", 1536),
                       ("zin", 512), ("zz", 256),
                       ("ct", 512),
                       ("cl", 512),
                       ("fe", 520),
                       ("rm8", 128), ("vb", 128), ("cv", 1024),
                       ("bt", 1024),
                       ("vt", 1024)):
        s[name] = ("sbuf", [128, cols], "bfloat16")
    for name, cols in (("vi", 8), ("li", 128), ("fa", 8), ("fb", 8), ("sca", 4), ("scb", 4), ("m16", 128),
                       ("pf", 4), ("k2", 16), ("pm", 264), ("junk", 264),
                       ("cnt", 4), ("g1", 4), ("g2", 4), ("lrow", 768), ("lsc", 256), ("yo", 256)):
        s[name] = ("sbuf", [128, cols], "float32")
    for name, cols in (("yi", 128), ("yb", 128), ("pint", 4), ("pa7", 4)):
        s[name] = ("sbuf", [128, cols], "int32")
    for name, cols in (("coff", 16), ("roff", 8), ("loff", 48)):
        s[name] = ("sbuf", [128, cols], "uint16")
    pairs = [("uq", "us", 144), ("sq", "ss", 384), ("zq", "zs", 128), ("cq", "cs", 128), ("lq", "ls", 128),
             ("eq", "es", 512), ("bq", "bs", 256)]
    pairs += [("xq%d" % t, "xs%d" % t, X0 + TC) for t in range(R + 1)]
    pairs += [("%sq%d" % (n, t), "%ss%d" % (n, t), 256) for t in range(R) for n in ("la", "ro", "vv", "vp")]
    for q, p, cols in pairs:
        s[q] = ("sbuf", [128, cols], Q8)
        s[p] = ("sbuf", [128, cols], "uint8")
    s["pa"] = ("psum", [128, 2048], "float32")
    s["pb"] = ("psum", [128, 2048], "float32")
    return s


SCRATCH = _scratch()
SEMAPHORES = (["sv", "sa", "sp", "sg", "lw", "lxa", "lxb", "lz", "sto", "sent"]
              + ["arrc%d" % t for t in range(R)] + ["arrs%d" % t for t in range(R)])


def rank_program(g, core, T, topo):
    rank = T.rank_of(core)
    if rank is None:
        return
    A = AluOpType
    F = ActivationFunctionType
    cores = list(T.cores)
    n = len(cores)
    queues = {"V": g.vector, "S": g.scalar, "P": g.tensor, "G": g, "Y": g.sync}
    count = {}
    waited = {q: {} for q in queues}

    def wait(q, *deps):
        need = {}
        for d in deps:
            if d is not None:
                need[d[0]] = max(need.get(d[0], 0), d[1])
        for s, c in need.items():
            if waited[q].get(s, 0) < c:
                queues[q].wait_ge(T.sem[s], c)
                waited[q][s] = c

    def done(ins, s, k=1):
        ins.then_inc(T.sem[s], k)
        count[s] = count.get(s, 0) + k
        return (s, count[s])

    def ts(out, in0, s1, s2, op0, op1=None, deps=()):
        wait("V", *deps)
        if op1 is None:
            return done(g.vector.tensor_scalar(out, in0, s1, None, op0), "sv")
        return done(g.vector.tensor_scalar(out, in0, s1, s2, op0, op1), "sv")

    def cp(out, in_, deps=()):
        wait("V", *deps)
        return done(g.vector.tensor_copy(out, in_), "sv")

    def ms(out, c, deps=()):
        wait("V", *deps)
        return done(g.vector.memset(out, c), "sv")

    def red(out, in_, op, deps=()):
        wait("V", *deps)
        return done(g.vector.tensor_reduce(out, in_, AxisListType.X, op), "sv")

    def scan(out, d0, d1, init, op0, op1, deps=()):
        wait("V", *deps)
        return done(g.vector.tensor_tensor_scan(out, d0, d1, init, op0, op1), "sv")

    def qz(q, s, in_, deps=()):
        wait("V", *deps)
        return done(g.vector.quantize_mx(q, s, in_), "sv")

    def act(out, in_, func, deps=(), **kw):
        wait("S", *deps)
        return done(g.scalar.activation(out, in_, func, **kw), "sa")

    def mm(out, lq, ls, a, rq, rs, b, start, stop, deps=()):
        wait("P", *deps)
        return done(g.tensor.matmul_mx(out, lq[:, a:a + 128], ls[:, a:a + 128], rq[:, b:b + 128], rs[:, b:b + 128],
                                       start, stop), "sp")

    def iota(out, pattern, base, cm, small, deps=()):
        wait("G", *deps)
        if small:
            return done(g.iota(out, pattern, base, cm, allow_small_or_imprecise_dtypes=True), "sg")
        return done(g.iota(out, pattern, base, cm), "sg")

    def dma(q, out, in_, s, deps=()):
        wait(q, *deps)
        return done(queues[q].dma_start(out, in_), s, 16)

    def pickq(out, win, off, deps=()):
        return cp(out.bitcast(dt.uint32), win.bitcast(dt.uint32).indirect(off), deps)

    def picks(out, win, off, deps=()):
        return act(out, win.indirect(off), F.Copy, deps)

    def bank(buf, b):
        return buf[:, 512 * b:512 * b + 128]

    def state(t, h, tile, deps):
        a, b = (Z0, X0 + 128) if h == 0 else (X0 + 128, X0 + TC)
        return qz(T["xq%d" % t][:, a:b], T["xs%d" % t][:, a:b], tile[:, 4 * (a - Z0):4 * (b - Z0)], deps)

    others = [cores[(rank + k) % n] for k in range(1, n)]
    lanes = [e for e in topo.engines(core, others[0]) if all(e in topo.engines(core, o) for o in others)]
    ids = [DstId(rid=topo.addr(o)[0], pnc=topo.addr(o)[1]) for o in others]

    def spread(view, sem, deps):
        wait("G", *deps)
        tr = RemoteDMATransfer(dst_ids=ids, dma_engine_mask=sum(1 << e for e in lanes), remote_sem=T.sem[sem],
                               srcs=[view()], dsts=[view() for o in others])
        g.remote_dma_fused([tr], local_sem=T.sem.sent)
        count["sent"] = count.get("sent", 0) + len(lanes)
        return (sem, len(lanes) * (n - 1))

    BIT = 2.0 ** 30
    PEN = 2.0 ** 42
    LOW = -(2.0 ** 70)
    UNP = -0.0625

    t_xa = dma("S", T.xin[:, 8:520], T.x[:, 0:512], "lxa")
    t_w = dma("Y", T.ut[:, 0:96], T.w[:, 0:96], "lw")
    t_xb = dma("Y", T.xin[:, 520:1032], T.x[:, 512:1024], "lxb")
    t_z = dma("Y", T.zin[:], T.z[:], "lz", [t_xb])

    i_v = iota(T.vi[0:32, 0:4], [[1, 4]], 2, -1, True)
    i_l = iota(T.li[0:32, :], [[16, 2], [0, 4], [1, 16]], 0, 0, True)

    t_zz = ms(T.zz[:], 0.0)
    ms(T.bt[:, 0:1024:4], 0.0)
    t_b1 = ms(T.bt[:, 1:1024:4], BIT)
    wait("G", t_b1)
    i_sel = done(g.affine_select(T.bt[64:96, 0:1024:4], T.bt[64:96, 1:1024:4], [[0, 16], [1, 16]], A.is_equal, 0.0,
                                 0, -1), "sg")
    i_vb = iota(T.vb[:], [[1, 128]], 0, -1, True, [i_sel])
    iota(T.pint[:, 0:1], [[0, 1]], 0, 257, False)
    i_m = iota(T.m16[:], [[0, 8], [100, 16]], 0, 0, True)
    i_k = iota(T.k2[:], [[2, 16]], 0, 0, True)
    i_k = iota(T.k2[64:128, :], [[-16, 2], [2, 8]], 16, 0, True, [i_k])

    act(T.ut[:, 96:336], T.zz[:, 0:240], F.Copy, [t_zz])
    s_ut = act(T.ut[:, 336:576], T.zz[:, 0:240], F.Copy)
    act(T.bt[:, 2:1024:4], T.zz[:], F.Copy)
    s_bt = act(T.bt[:, 3:1024:4], T.zz[:], F.Copy)
    act(T.cl[:, 0:256], T.zz[:], F.Copy)
    s_cl = act(T.cl[:, 256:512], T.zz[:], F.Copy)
    a0 = ts(T.fa[0:32, 0:4], T.vi[0:32, 0:4], 2.0, 1.0, A.min, A.max, [i_v])
    a1 = ts(T.fa[0:32, 4:5], T.vi[0:32, 3:4], 1.0, PEN / 8, A.is_ge, A.mult)
    t_xt = ms(T.xin[:, 0:8], 0.0)
    ms(T.pm[:, 0:2], LOW)
    a2 = red(T.sca[0:32, 0:1], T.fa[0:32, 0:5], A.mult, [a0, a1])
    t_pm = ms(T.pm[:, 132:134], LOW)
    t_ht = ms(T.ht[:, 0:8], 0.0)
    a3 = ts(T.yi[0:32, :], T.li[0:32, :], T.sca[0:32, 0:1], 8 / PEN, A.mult, A.mult, [a2, i_l])
    t_ct = ms(T.ct[:], 0.0)
    a4 = ts(T.yb[0:32, :], T.yi[0:32, :], 16, None, A.bitwise_and, None, [a3])
    b0 = ts(T.fb[0:32, 0:4], T.vi[0:32, 0:4], 2.0, 1.0, A.is_lt, A.add)
    b1 = ts(T.fb[0:32, 4:5], T.vi[0:32, 3:4], 1.0, 1.0 / (BIT * BIT), A.is_ge, A.mult)
    r0 = ms(T.rm8[:], 1.0)
    c0 = ts(T.ct[0:32, 0:512:4], T.yb[0:32, :], -8.0, T.fa[0:32, 4:5], A.add, A.mult, [a4, t_ct])
    c1 = ts(T.ct[0:32, 1:512:4], T.yb[0:32, :], -PEN / 16, None, A.mult)
    b2 = red(T.scb[0:32, 0:1], T.fb[0:32, 0:5], A.mult, [b0, b1])
    t_rm8 = ms(T.rm8[:, 0:128:8], 0.0, [r0])
    t_cq = qz(T.cq[:], T.cs[:], T.ct[:], [c0, c1])

    def repeat(t):
        tok = None
        for e in range(4):
            col = 4 * (8 * t + 6) + e
            tok = act(T.st[:, 512 * t + e:512 * t + 512:4], T.zz[:, 0:128], F.Identity, [t_w],
                      bias=T.ut[:, col:col + 1])
        return tok

    s_r0 = repeat(0)
    lc = [act(T.cl[0:32, 0:512:4], T.bt[0:32, 1:512:4], F.Identity, [s_cl, b2], scale=T.scb[0:32, 0:1]),
          act(T.cl[64:96, 0:512:4], T.bt[64:96, 0:512:4], F.Copy, [i_sel], scale=64.0 / (BIT * BIT))]
    t_uq = qz(T.uq[:], T.us[:], T.ut[:], [t_w, s_ut])
    x_a = state(0, 0, T.xin, [t_xa, t_xt])
    x_b = state(0, 1, T.xin, [t_xb])
    t_sq = qz(T.sq[:, 0:128], T.ss[:, 0:128], T.st[:, 0:512], [s_r0])

    late = {}
    for t in range(R):
        xq, xs = T["xq%d" % t], T["xs%d" % t]
        laq, las = T["laq%d" % t], T["las%d" % t]
        roq, ros = T["roq%d" % t], T["ros%d" % t]
        vvq, vvs = T["vvq%d" % t], T["vvs%d" % t]
        vpq, vps = T["vpq%d" % t], T["vps%d" % t]
        pe, pl = (T.pa, T.pb) if t % 2 == 0 else (T.pb, T.pa)

        p_pl = [mm(bank(pe, h), T.uq, T.us, 8 * t, xq, xs, X0 + 128 * h, True, True, [t_uq, (x_a, x_b)[h]])
                for h in range(2)]
        for h in range(2):
            mm(bank(pe, 2 + h), T.sq, T.ss, 128 * t, xq, xs, X0 + 128 * h, True, False, [t_sq])
        v_lt = [ts(T.bt[0:32, 512 * h:512 * h + 512:4], pe[0:32, 512 * h:512 * h + 128], 0.0, BIT, A.is_lt, A.mult,
                   [p_pl[h]]) for h in range(2)]
        v_bq = [qz(T.bq[:, 128 * h:128 * h + 128], T.bs[:, 128 * h:128 * h + 128], T.bt[:, 512 * h:512 * h + 512],
                   [v_lt[h], s_bt, i_sel]) for h in range(2)]
        p_pen = [mm(bank(pe, 2 + h), T.cq, T.cs, 0, T.bq, T.bs, 128 * h, False, True, [v_bq[h], t_cq])
                 for h in range(2)]
        if t == 0:
            t_fe0 = ms(T.fe[:], 0.0)
        v_pm, s_cnt = [], []
        for h in range(2):
            at = 132 * h
            v_pm.append(scan(T.pm[:, at + 2:at + 130], bank(pe, 2 + h), T.zz[:, 0:128], LOW, A.max, A.add,
                             [p_pen[h], t_pm]))
            s_cnt.append(act(T.junk[:, at:at + 130], T.pm[:, at:at + 130], F.Sign, [v_pm[h]],
                             bias=T.pm[:, at + 129:at + 130], scale=-1.0, accum_out=T.cnt[:, h:h + 1]))
        if t == 0:
            t_fe = ts(T.fe[:, 3:515:4], T.vb[:], 0.0, UNP, A.is_equal, A.mult, [t_fe0, i_vb])
        v_g1 = ts(T.g1[:, 0:1], T.pm[:, 261:262], T.pm[:, 129:130], Z0 + 128.0, A.is_gt, A.mult, v_pm)
        v_g2 = ts(T.g2[:, 0:1], T.cnt[:, 0:1], float(Z0), None, A.add, None, [s_cnt[0]])
        v_ro = None
        for col, a, b, w in ((0, 0, 0, 128), (1, 0, 64, 64), (1, 64, 0, 64)):
            v_ro = ts(T.roff[a:a + w, 2 * t + col:2 * t + col + 1], T.cnt[b:b + w, 1:2], T.g1[b:b + w, 0:1],
                      T.g2[b:b + w, 0:1], A.add, A.max, [v_g1, v_g2, s_cnt[1]])
        lo, hi = NL * rank, NL * rank + NL
        v_pk = pickq(laq[:, lo:hi], xq[:], T.roff[:, 2 * t:2 * t + 2], [v_ro])
        s_pk = picks(las[:, lo:hi], xs[:], T.roff[:, 2 * t:2 * t + 2], [v_ro])

        a_c = spread(lambda: laq[:, lo:hi].bitcast(dt.uint8), "arrc%d" % t, [v_pk])
        a_s = spread(lambda: las[:, lo:hi], "arrs%d" % t, [s_pk])

        if t == 0:
            k0 = ts(T.pa7[:, 0:1], T.pint[:, 0:1], 3, 225, A.logical_shift_right, A.bitwise_and, [i_k])
            late["lq"] = qz(T.lq[:], T.ls[:], T.cl[:], lc)
            k1 = cp(T.pf[:, 0:1], T.pa7[:, 0:1], [k0])
            for b in range(4):
                late["eq"] = qz(T.eq[:, 128 * b:128 * b + 128], T.es[:, 128 * b:128 * b + 128],
                                T.fe[:, 3 - b:515 - b], [t_fe])
            late["coff"] = ts(T.coff[:], T.k2[:], T.pf[:, 0:1], None, A.add, None, [k1])
            repeat(1)
            late["st"] = repeat(2)
        p_l = [mm(bank(pl, h), T.lq, T.ls, 0, T.bq, T.bs, 128 * h, True, True, [late["lq"]]) for h in range(2)]
        l_s = [scan(T.lsc[:, 128 * h:128 * h + 128], T.m16[:], bank(pl, h), 0.0, A.min, A.max, [p_l[h], i_m])
               for h in range(2)]
        s_l = [act(T.lrow[0:1, 256 * t + 128 * h:256 * t + 128 * h + 128],
                   pl[0:1, 512 * h:512 * h + 128], F.Copy, [l_s[h]]) for h in range(2)]
        if t == 0:
            t_sq = qz(T.sq[:, 128:384], T.ss[:, 128:384], T.st[:, 512:1536], [late["st"]])
        if t == 1:
            late["zq"] = qz(T.zq[:], T.zs[:], T.zin[:], [t_z])
        v_lo = ts(T.loff[:, 16 * t:16 * t + 16], T.lsc[:, 15:256:16], 8.0, 7.0 - 512.0, A.mult, A.add, l_s)
        if t == R - 1:
            s_lv = act(T.lrow[0:1, 0:768:16], T.lrow[0:1, 0:768:16], F.Identity, s_l, bias=-64.0)
            dma("Y", T.lv[:], T.lrow[0:1, 0:768], "sto", [s_lv])

        pickq(roq[:, 0:128], laq[:], T.coff[:, 0:8], [a_c, late["coff"], v_pk])
        pickq(roq[:, 128:256], laq[:], T.coff[:, 8:16])
        put = [[cp(ros[:, 0:128], las[:].indirect(T.coff[:, 0:8]), [a_s, s_pk])] + s_l,
               [picks(ros[:, 128:256], las[:], T.coff[:, 8:16], [a_s, late["coff"], s_pk])]]
        p_d, freed, sums = {}, {}, {}
        for k in range(8):
            h, b = divmod(k, 4)
            p_d[k] = mm(bank((pl, pe)[h], b), T.eq, T.es, 128 * b, roq, ros, 128 * h, True, True,
                        put[h] + [late["eq"]])
            if k in VIA:
                freed[k] = act(T.cv[:, 128 * k:128 * k + 128], bank((pl, pe)[h], b), F.Copy, [p_d[k]])
        for k in ORDER_V:
            h, b = divmod(k, 4)
            dst = T.vt[:, 512 * h + b:512 * h + 512:4]
            if k in VIA:
                sums[k] = scan(dst, T.rm8[:], T.cv[:, 128 * k:128 * k + 128], 0.0, A.mult, A.add, [freed[k]])
            else:
                sums[k] = freed[k] = scan(dst, T.rm8[:], bank((pl, pe)[h], b), 0.0, A.mult, A.add, [p_d[k], t_rm8])
        v_vq = None
        for h in range(2):
            v_vq = qz(vvq[:, 128 * h:128 * h + 128], vvs[:, 128 * h:128 * h + 128], T.vt[:, 512 * h:512 * h + 512],
                      [sums[4 * h + b] for b in range(4)])
        for k in range(8):
            h, b = divmod(k, 4)
            mm(bank((pl, pe)[h], b), T.eq, T.es, 128 * b, xq, xs, X0 + 128 * h, True, False, [freed[k]])

        picked = []
        for h in range(2):
            off = T.loff[:, 16 * t + 8 * h:16 * t + 8 * h + 8]
            picked.append([pickq(vpq[:, 128 * h:128 * h + 128], vvq[:], off, [v_vq, v_lo]),
                           picks(vps[:, 128 * h:128 * h + 128], vvs[:], off, [v_vq, v_lo])])
        last = t == R - 1
        outs = [[t_ht], []]
        for h in range(2):
            ps = (pl, pe)[h]
            for b in range(4):
                p_s = mm(bank(ps, b), T.eq, T.es, 128 * b, vpq, vps, 128 * h, False, True, picked[h])
                dst = T.ht[:, 8 + 512 * h + b:520 + 512 * h:4]
                if (h, b) in STEP_V[last]:
                    outs[h].append(ts(dst, bank(ps, b), 1 / UNP, None, A.mult, None, [p_s]))
                else:
                    outs[h].append(act(dst, bank(ps, b), F.Copy, [p_s], scale=1 / UNP))
            if h == 1 - last:
                x_a = state(t + 1, 0, T.ht, outs[0])
        x_b = state(t + 1, 1, T.ht, outs[1])

    xq, xs = T["xq%d" % R], T["xs%d" % R]
    pe = T.pa if R % 2 == 0 else T.pb
    p_ya = mm(bank(pe, 0), T.zq, T.zs, 0, xq, xs, X0, True, True, [x_a, late["zq"]])
    p_yb = mm(bank(pe, 1), T.zq, T.zs, 0, xq, xs, X0 + 128, True, True, [x_b])
    dma("Y", T.oc[:, 0:512], xq[:, X0:X0 + 128].bitcast(dt.uint8), "sto", [x_a])
    s_ya = act(T.yo[:, 0:128], bank(pe, 0), F.Copy, [p_ya])
    dma("S", T.y[:, 0:128], T.yo[:, 0:128], "sto", [s_ya])
    dma("Y", T.oc[:, 512:1024], xq[:, X0 + 128:X0 + TC].bitcast(dt.uint8), "sto", [x_b])
    for k in range(4):
        dma("Y" if k < 2 else "S", T.osc[4 * k:4 * k + 4, 0:TC], xs[32 * k:32 * k + 4, X0:X0 + TC], "sto", [x_b])
    v_yb = cp(T.yo[:, 128:256], bank(pe, 1), [p_yb])
    dma("Y", T.y[:, 128:256], T.yo[:, 128:256], "sto", [v_yb])
    wait("G", *[(s, count[s]) for s in ("sent", "sg", "sp", "sa", "sv")])
    wait("Y", ("sto", count["sto"]))
